import numpy as np, ml_dtypes
CORES = [2,6,10,14,18,22,26,30]
N = 8
BF = ml_dtypes.bfloat16
def gentries(a):
    return np.ascontiguousarray(a.reshape(8, 16, -1).transpose(0, 2, 1)).reshape(8, -1)
def gtable(e):
    e = np.asarray(e); return np.ascontiguousarray(e.reshape(8, -1, 16).transpose(0, 2, 1)).reshape(128, -1).astype(np.int32)
V, G, P, E, O, RO, ST = 2048, 256, 2048, 144, 16, 2, 4
W = V + (N - 1) * G; L = E + (N - 1) * O
def power(rng, *shape):
    lead = rng.integers(0, 16, shape[:-2] + (1,) + shape[-1:])
    return np.where(np.arange(16)[:, None] == lead, rng.integers(128, 256, shape), rng.integers(0, 40, shape))
def parts(rng):
    x = power(rng, N, 8, 16, V); plans = power(rng, 8, 16, P)
    share = 0.3 + 0.3 * rng.random((N, 8, 1, 1))
    nb = np.where(rng.random((N, 8, 16, V)) < share, rng.integers(V, W, (N, 8, 16, V)), rng.integers(0, V, (N, 8, 16, V)))
    pt = 2048 * rng.integers(0, 1024, (N, 8, 16, V)) + rng.integers(0, P, (N, 8, 16, V))
    req = np.ascontiguousarray(np.argsort(rng.random((N, 8, RO, V)), axis=-1)[..., :E])
    th = rng.integers(180, 281, (N, 8, 16, 1))
    return x, nb, pt, plans, req, th
def pack(x, nb, pt, plans, req, th):
    return {"x": np.ascontiguousarray(x.reshape(N, 128, V)).astype(np.float32).astype(BF), "nb": np.ascontiguousarray(nb.reshape(N, 128, V)).astype(np.int32),
            "pt": np.ascontiguousarray(pt.reshape(N, 128, V)).astype(np.int32), "plans": np.repeat(plans.reshape(1, 128, P), N, axis=0).astype(np.float32).astype(BF),
            "req": np.stack([gtable(a.reshape(8, RO * E)) for a in req]), "th": np.ascontiguousarray(th.reshape(N, 128, 1)).astype(np.int32)}
def setup_inputs(rng):
    return pack(*parts(rng))
def setup_inputs_room(rng):
    x, nb, pt, plans, req, th = parts(rng); x = np.maximum(x, 1); plans = np.maximum(plans, 1); th = th * 0
    for q in range(N):
        for g in range(8):
            o = rng.permutation(V)[:E]; req[q, g, 0] = o
            n = [int(a) for a in rng.choice(np.array([0, 1, O - 1, O, O + 1]), N - 1)]
            if q == 0: n[0] = (O, O + 1, O - 1, 0, 1, O, O + 1, E)[g]
            left = E; goals = []
            for d in range(N - 1):
                m = min(n[d], left); left -= m
                goals.append(V + d * G + rng.integers(0, G, m))
            goals.append(o[rng.integers(0, E, left)])
            nb[q, g][:, o] = rng.permutation(np.concatenate(goals))[None, :]
    return pack(x, nb, pt, plans, req, th)
def setup_inputs_ties(rng):
    x, nb, pt, plans, req, th = parts(rng)
    x = rng.integers(0, 4, x.shape); plans = rng.integers(0, 4, plans.shape); th = rng.integers(12, 19, th.shape)
    pt = 2048 * rng.integers(0, 4, pt.shape) + rng.integers(0, P, pt.shape)
    x[:, 0] = 5; x[:, 1] = 5; th[:, 0] = 80; th[:, 1] = 79; pt[:, :2] = pt[:, :2] & 2047
    x[:, 2, ::2] = 0; th[:, 2, ::2] = 0
    return pack(x, nb, pt, plans, req, th)
def setup_inputs_alike(rng):
    x, nb, pt, plans, req, th = parts(rng); s = np.arange(V)
    req[:, 0] = req[:, 0, :1]
    req[:, 3] = rng.integers(0, 40, (N, RO, E))
    req[:, 5] = rng.choice(np.array([0, V - 1, 1, V >> 1]), (N, RO, E))
    req[:, 7] = np.where(rng.random((N, RO, E)) < 0.5, req[:, 7, :, :1], req[:, 7])
    nb[:, 2] = np.where(rng.random((N, 16, V)) < 0.5, s, nb[:, 2])
    nb[:, 4] = rng.choice(np.array([0, V - 1, V, V + G - 1, W - 1]), (N, 16, V))
    nb[:, 6] = nb[:, 6, :1]
    nb[:, 1, 8:] = nb[:, 1, :8]
    return pack(x, nb, pt, plans, req, th)
def wire(rng, x, nb, plans, th, g, nxt):
    strong = np.zeros((N, V), bool)
    for q in range(N):
        t = nxt[q][nxt[q] >= 0]; strong[q, t[t < V]] = True
        e = t[t >= V] - V; strong[(q - 1 - e // G) % N, e % G] = True
    x[:, g] = np.where(strong[:, None, :], rng.integers(200, 256, (N, 16, V)), rng.integers(0, 8, (N, 16, V)))
    plans[g] = rng.integers(0, 8, (16, P)); th[:, g] = rng.integers(112, 200, (N, 16, 1))
    for q in range(N):
        seen = np.concatenate([strong[q]] + [strong[(q - d) % N, :G] for d in range(1, N)]); calm = np.nonzero(~seen)[0]
        nb[q, g] = calm[rng.integers(0, len(calm), (16, V))]
        s = np.nonzero(nxt[q] >= 0)[0]; nb[q, g][rng.integers(0, 16, len(s)), s] = nxt[q, s]
def ordered(rng, nxt, pt, req, g, a, goals, ban):
    for d in range(1, N):
        q = (a + d) % N; o = rng.permutation(V); s = o[:O]
        nxt[q, s] = V + (d - 1) * G + goals[d - 1]
        cost = np.where(np.arange(16)[:, None] == ban[d - 1][None, :], 0, rng.integers(500, 1024, (16, O)))
        pt[q, g][:, s] = 2048 * cost + (pt[q, g][:, s] & 2047)
        req[q, g, 0] = rng.permutation(o[:E]); req[q, g, 1:] = rng.choice(o[O:], (RO - 1, E))
def setup_inputs_hubs(rng):
    x, nb, pt, plans, req, th = parts(rng)
    for q in range(N):
        for g in range(8):
            own = np.concatenate([rng.permutation(G)[:3], rng.permutation(V)[:3]])
            x[q, g][:, own] = 255 - rng.integers(0, 3, (16, 6))
            goals = np.concatenate([own, V + rng.integers(0, (N - 1) * G, 2)])
            nb[q, g] = np.where(rng.random((16, V)) < 0.08, rng.choice(goals, (16, V)), nb[q, g])
    n = (N - 1) * O
    for g in (4, 5, 6):
        a = int(rng.integers(0, N)); nxt = np.full((N, V), -1, np.int64)
        goals = np.concatenate([np.zeros(1, np.int64), 1 + rng.permutation(G - 1)[:n - 1]]); ban = rng.integers(0, 16, n); ban[0] = 0
        o = rng.permutation(np.setdiff1d(np.arange(V), goals))
        ordered(rng, nxt, pt, req, g, a, goals.reshape(N - 1, O), ban.reshape(N - 1, O))
        if g == 4:
            m = 2 * E * ST; c = o[:m].reshape(2 * E, ST); nxt[a, c[:, :-1]] = c[:, 1:]
            e = np.concatenate([goals[:, None], o[m:m + n * (ST - 1)].reshape(n, ST - 1)], axis=1); nxt[a, e[:, :-1]] = e[:, 1:]
            req[a, g] = rng.choice(o[m + n * (ST - 1):], (RO, E)); req[a, g, 0] = c[:E, 0]; req[a, g, 1] = c[E:, 0]
        elif g == 5:
            hub = o[:RO]; block = o[RO:RO + (RO - 1) * E].reshape(RO - 1, E)
            nxt[a, block] = hub[:RO - 1, None]; nxt[a, goals] = hub[1]
            req[a, g, :RO - 1] = block; req[a, g, RO - 1] = rng.permutation(np.concatenate([goals, block[-1]]))[:E]
        else:
            b = o[:n]; nxt[a, goals] = b; nxt[a, b] = goals
            c = o[n:n + E]; e = o[n + E:n + 2 * E]; nxt[a, c] = e; nxt[a, e] = c
            req[a, g] = rng.choice(o[n + 2 * E:], (RO, E)); req[a, g, 0] = c
        wire(rng, x, nb, plans, th, g, nxt)
        if g == 6:
            x[a, g][ban, b] = rng.integers(0, 8, n)
            cost = np.where(np.arange(16)[:, None] == ban[None, :], 1023, rng.integers(0, 301, (16, n)))
            pt[a, g][:, b] = 2048 * cost + (pt[a, g][:, b] & 2047)
    return pack(x, nb, pt, plans, req, th)
def setup_inputs_spread(rng):
    x, nb, pt, plans, req, th = parts(rng)
    x = np.minimum((np.exp2(8 * rng.random((N, 8, 1, V))) * rng.random((N, 8, 16, V))).astype(np.int64), 255)
    plans = np.minimum((np.exp2(8 * rng.random((8, 1, P))) * rng.random((8, 16, P))).astype(np.int64), 255)
    x[..., 0] = 255; x[..., V - 1] = 255
    cost = np.minimum(np.exp2(10 * rng.random(pt.shape)).astype(np.int64) - 1, 1023)
    pt = 2048 * cost + rng.integers(0, P, pt.shape); pt[..., 0] = 2048 * 1023 + P - 1
    th = (np.exp2(5 + 5 * rng.random((N, 8, 1, 1))) * (0.5 + rng.random((N, 8, 16, 1)))).astype(np.int64)
    th[:, 0] = rng.integers(0, 4081, (N, 16, 1))
    for g, n, lo, t0, t1, u0, u1, k0, k1 in ((5, 8, 200, 3900, 4080, 0, 12, 500, 200), (6, 15, 240, 3000, 3700, 22, 26, 900, 300), (7, 16, 240, 3930, 3990, 0, 0, 500, 0)):
        heavy = rng.permutation(16)[:, None] < n
        x[:, g] = np.where(heavy, rng.integers(lo, 256, (N, 16, V)), rng.integers(0, 4, (N, 16, V)))
        plans[g] = np.where(heavy, rng.integers(lo, 256, (16, P)), rng.integers(0, 4, (16, P)))
        th[:, g] = np.where(heavy, rng.integers(t0, t1 + 1, (N, 16, 1)), rng.integers(u0, u1 + 1, (N, 16, 1)))
        cost = np.where(heavy, rng.integers(k0, 1024, (N, 16, V)), rng.integers(0, k1 + 1, (N, 16, V)))
        pt[:, g] = 2048 * cost + (pt[:, g] & 2047)
    return pack(x, nb, pt, plans, req, th)
def check_inputs(d):
    bad = []
    for k in ("x", "plans"):
        v = np.asarray(d[k]).astype(np.float32)
        if not (np.min(v) >= 0 and np.max(v) <= 255 and np.all(v == np.floor(v))): bad.append("range of " + k)
    for k, hi in (("nb", W - 1), ("pt", 2048 * 1023 + 2047), ("req", V - 1), ("th", 4080)):
        if not (np.min(d[k]) >= 0 and np.max(d[k]) <= hi): bad.append("range of " + k)
    if np.max(np.asarray(d["pt"]).astype(np.int64) & 2047) >= P: bad.append("plan numbers in pt")
    v = np.asarray(d["plans"]).astype(np.float32)
    if not np.all(v == v[:1]): bad.append("plans alike on all ranks")
    return bad
def chains(w, nbg, ptg, tg, frozen, first, ban):
    lanes = np.arange(L); ch = np.arange(16)[:, None]; mark = np.array(frozen)
    got = np.zeros((ST, L), bool); where = np.zeros((ST, L), np.int64); plan = np.zeros((ST, L), np.int64)
    good = np.zeros(L, bool); order = np.full(L, -1, np.int64); live = first >= 0; s = first
    for k in range(ST):
        at = np.where(live, s, 0)
        idx = np.nonzero(live & ~mark[at])[0]
        u, j = np.unique(at[idx], return_index=True)
        reach = np.zeros(L, bool); reach[idx[j]] = True; mark[u] = True
        q = nbg[:, at]
        p = w[:, q]
        total = np.add.reduce(p, axis=1); over = total > tg
        price = total + (ptg[:, at] >> 11) + 4096 * over + 16384 * (ch == ban[None, :])
        c = np.argmin(price, axis=0)
        got[k] = reach; where[k] = at; plan[k] = ptg[c, at] & 2047
        stuck = over[c, lanes]
        b = q[np.argmax(p[c, :, lanes], axis=1), lanes]
        good = good | (reach & ~stuck)
        order = np.where(reach & stuck & (b >= V), (b - V) * 16 + c, order)
        live = reach & stuck & (b < V); s = b; ban = c
    return got, where, plan, good, order
def reference(x, nb, pt, plans, req, th):
    now = x.astype(np.float32).astype(np.int64).reshape(N, 8, 16, V); nbl = nb.astype(np.int64).reshape(N, 8, 16, V); ptl = pt.astype(np.int64).reshape(N, 8, 16, V)
    pl = plans.astype(np.float32).astype(np.int64).reshape(N, 8, 16, P); t = th.astype(np.int64).reshape(N, 8, 16, 1)
    rq = np.stack([gentries(a) for a in req]).astype(np.int64).reshape(N, 8, RO, E)
    frozen = np.zeros((N, 8, V), bool); inbox = np.full((N, 8, N - 1, O), -1, np.int64)
    for rnd in range(RO):
        new = np.array(now); nextbox = np.full((N, 8, N - 1, O), -1, np.int64)
        for r in range(N):
            w = np.concatenate([now[r]] + [now[(r - d) % N][:, :, :G] for d in range(1, N)], axis=2)
            for g in range(8):
                box = inbox[r, g].reshape(-1)
                first = np.concatenate([rq[r, g, rnd], np.where(box >= 0, box >> 4, -1)])
                ban = np.concatenate([np.full(E, -1, np.int64), np.where(box >= 0, box & 15, -1)])
                got, where, plan, good, order = chains(w[g], nbl[r, g], ptl[r, g], t[r, g], frozen[r, g], first, ban)
                for d in range(1, N):
                    i = np.nonzero((order >= (d - 1) * 16 * G) & (order < d * 16 * G))[0][:O]
                    good[i] = True; nextbox[(r - d) % N, g, d - 1, :len(i)] = order[i] - (d - 1) * 16 * G
                for k in range(ST):
                    m = got[k] & good
                    new[r, g][:, where[k][m]] = pl[r, g][:, plan[k][m]]
                frozen[r, g][where[0][got[0] & ~good]] = True
        now = new; inbox = nextbox
    return {"y": now.reshape(N, 128, V).astype(np.float32).astype(BF)}

@@ -1,0 +1,668 @@
+import numpy as np
+from concourse.bass import DstId, RemoteDMATransfer
+from concourse.mybir import AluOpType as OP
+from concourse.mybir import ActivationFunctionType as AF
+
+V, G, W, NR = 2048, 256, 3840, 8
+PL0, OWN, GH, GR, TB1, WEND = 1, 2064, 4112, 5904, 7952, 11792
+F32, BF, F16, I32, U16 = "float32", "bfloat16", "float16", "int32", "uint16"
+SMALL = {"MK": 16, "WF": 16, "W25": 16, "WI": 64, "KM": 16, "FM": 80, "THR": 16, "RE": 64, "LV": 80, "OV": 64, "E1": 64,
+         "PLW": 64, "GD": 64, "AM": 48, "GO": 16, "VAL": 64, "FZ": 16, "OO": 64, "O2": 64, "RKC": 16, "PAY": 32, "O4": 48}
+BUFS = {
+    I32: {"NB": V, "PT": V, "REQ": 32, "TH": 4, "PB": 8, "HI5": 16, "RI": 64, "PX0": 256, "PX1": 256, "CST": 256, "MI": 16,
+          "I2": 32, "BI": 16, "I3": 32, "E2": 64, "E3": 64, "DD": 32, "O3": 32},
+    BF: {"WIN": WEND, "Y": V, "XT": W, "I1": 128, "IK": 128, "IH": 128, "SW": (4, 128), "I21": 128, "SELD": 64,
+         "MKD": 16, "TRI": 128, "ONE": 128, "SELF": 16, "SELC": 8, "RMIN": 256, "EE": 32, "IA": 240, "P0": 4096, "P1": 4096,
+         "T0": 4096, "T1": 4096, "SG": 256, "OH0": 256, "OH1": 256, "OB": 112, "X0": 256, "X1": 256, "ZW": 1024, "OA": 8192,
+         "ZF": 256, "TS": 128, "TW": 240, "M01": 128, "PR": 256, "IND": 128, "LVB": 128, "INP": 128, "N01": 128,
+         "ZO": (128, 16), "ZZ": 128, "PIB": 256},
+    U16: {"LAND": 224, "MSG": 32, "L16": 64, "L8": 8, "LK": 4, "BL": 320, "QL": 160, "Q0": 256, "Q1": 256, "OL0": 32,
+          "OL1": 32, "CL": 8, "IX": 128},
+    F16: {"LOW": 256, "QF": 256, "ZV": 1024},
+    F32: {"SF": sum(SMALL.values()), "PF": 8, "DM": 128, "JF": 256, "IF": 128, "SELP": 8, "RMAX": 256, "R8": 128, "DI": 128,
+          "JI": 128, "KB": 128, "K0": 128, "K1": 128, "THC": 1, "QS": 256, "SU": 256, "KEY": (8, 2, 16), "KT": 256, "SC": 256,
+          "K2": 256, "K2T": 256, "SC2": 256, "PS": 256, "FH": (5, 2, 2, 8), "PH": (4, 2, 2, 8), "CI": 128, "RK": 128,
+          "PTS": 128, "X3": 128, "OS": (2, 4, 16)},
+}
+SCRATCH = {n: ("sbuf", [128] + (list(s) if isinstance(s, tuple) else [s]), d) for d, b in BUFS.items() for n, s in b.items()}
+SCRATCH.update({n: ("psum", [128, 512], F32) for n in ("S0", "S1", "F1", "TT", "TM", "OC", "SM")})
+SCRATCH["QQ"] = ("psum", [128, 16, 2, 16], F32)
+SEMAPHORES = ["sv", "sa", "sp", "sg", "arr0", "arr1", "out0", "out1"] + ["d%d" % i for i in range(12)]
+HUGE = 2.0 ** 58
+BAN = 2.0 ** 24
+PE_CYC, SLACK, TRIES = 0.5, 40, 1200
+BLOCKS = (((0, 2), (2, 5)), ((0, 4), (4, 8)))
+DVE_CHUNKS = {(0, 0): (1,), (1, 0): (1, 3)}
+ORDER = {}
+
+
+def build(g, T, rank, topo):
+    nodes = []
+    sgs = []
+    hist = {}
+    grids = {}
+    place = {}
+    for n_, w_ in SMALL.items():
+        place[n_] = sum(SMALL[m_] for m_ in place)
+
+    def A(name, *idx):
+        if name in SMALL:
+            a, b, st = (idx[0] if idx else slice(None)).indices(SMALL[name])
+            name, idx = "SF", (slice(place[name] + a, place[name] + b, st if st > 1 else None),)
+        where, shape, d = SCRATCH[name]
+        if name not in grids:
+            grids[name] = np.arange(int(np.prod(shape[1:]))).reshape(shape[1:])
+        sel = grids[name][idx].ravel() if idx else grids[name].ravel()
+        bits = np.zeros(grids[name].size, np.uint8)
+        bits[sel] = 1
+        m = int.from_bytes(np.packbits(bits).tobytes(), "big")
+        ap = T[name][(slice(None),) + idx] if idx else T[name][:]
+        return {"ap": ap, "acc": [(name, m)], "n": len(sel), "two": d in (BF, F16, U16), "ps": where == "psum", "ind": False}
+
+    def C(name, a, b=None, st=None):
+        return A(name, slice(a, a + 1 if b is None else b, st))
+
+    def D(name, a, n):
+        return C(name, a, a + n)
+
+    ALL = slice(None)
+
+    def IND(win, off):
+        return {"ap": win["ap"].indirect(off["ap"]), "acc": win["acc"] + off["acc"], "n": off["n"] * 16,
+                "two": False, "ps": False, "ind": True}
+
+    def node(eng, cost, emit, rd, wr, sem=None, cnt=0, after=()):
+        k = len(nodes)
+        deps = {}
+        acc = [(name, m, w) for ops, w in ((rd, False), (wr, True)) for o in ops if isinstance(o, dict) for name, m in o["acc"]]
+        for name, m, w in acc:
+            ps = SCRATCH[name][0] == "psum"
+            for j, mj, wj in hist.get(name, ()):
+                if ps and nodes[j]["eng"] != eng:
+                    deps[j] = True
+                elif (w or wj) and (m & mj):
+                    deps[j] = deps.get(j, False) or not (ps and eng == "P")
+        for j in after:
+            deps.setdefault(j, False)
+        lab = wr[0]["acc"][0][0] if wr and isinstance(wr[0], dict) else "-"
+        nodes.append({"eng": eng, "cost": cost, "emit": emit, "deps": deps, "sem": sem, "cnt": cnt, "lab": lab})
+        for name, m, w in acc:
+            h = hist.setdefault(name, [])
+            if w and SCRATCH[name][0] != "psum":
+                h[:] = [e for e in h if e[1] & ~m]
+            h.append((k, m, w))
+        return k
+
+    def ap(o):
+        return o["ap"] if isinstance(o, dict) else o
+
+    def vcost(out, a, both=False):
+        if a["ind"]:
+            return 60 + 1.5 * a["n"]
+        return max(64, a["n"] * (2 if both else 0.5 if (out["two"] and a["two"]) else 1))
+
+    def cp(out, a):
+        return node("V", vcost(out, a), lambda: g.vector.tensor_copy(out["ap"], a["ap"]), [a], [out])
+
+    def tt(out, a, b, op):
+        c = vcost(out, a, True) if not (a["ps"] or b["ps"]) else max(64, a["n"])
+        return node("V", c, lambda: g.vector.tensor_tensor(out["ap"], a["ap"], b["ap"], op), [a, b], [out])
+
+    def ts(out, a, s1, op0, s2=None, op1=None):
+        def emit():
+            if op1 is None:
+                return g.vector.tensor_scalar(out["ap"], a["ap"], ap(s1), None, op0)
+            return g.vector.tensor_scalar(out["ap"], a["ap"], ap(s1), ap(s2), op0, op1)
+        return node("V", vcost(out, a), emit, [a, s1, s2], [out])
+
+    def ms(out, v):
+        return node("V", vcost(out, out), lambda: g.vector.memset(out["ap"], v), [], [out])
+
+    def scan(out, d0, d1, op0, op1):
+        return node("V", vcost(out, d1), lambda: g.vector.tensor_tensor_scan(out["ap"], d0["ap"], d1["ap"], 0.0, op0, op1), [d0, d1], [out])
+
+    def tr(out, a):
+        return node("V", vcost(out, a), lambda: g.vector.transpose(out["ap"], a["ap"]), [a], [out])
+
+    def rec(out, a):
+        return node("V", 230 + 6 * a["n"], lambda: g.vector.reciprocal(out["ap"], a["ap"]), [a], [out])
+
+    def act(out, a, func, bias=0.0, scale=1.0, extra=0, after=()):
+        c = (80 + 1.5 * a["n"] if a["ind"] else max(64, a["n"]) + 20) + extra
+        return node("A", c, lambda: g.scalar.activation(out["ap"], a["ap"], func, bias=ap(bias), scale=ap(scale)), [a, bias, scale], [out], after=after)
+
+    def gather(eng, out, src, after=()):
+        return cp(out, src) if eng == "V" else act(out, src, AF.Copy, after=after)
+
+    def mm(lst, after=()):
+        def emit():
+            for o, l, r, st, sp in lst:
+                ins = g.tensor.matmul(o["ap"], l["ap"], r["ap"], st, sp)
+            return ins
+        c = sum(max(min(64, l["n"]), r["n"]) * (1 if l["two"] else 4) for o, l, r, st, sp in lst) * PE_CYC + 40
+        return node("P", c, emit, [e[1] for e in lst] + [e[2] for e in lst], [e[0] for e in lst], after=after)
+
+    def grp(lst):
+        return [(o, l, r, i == 0, i == len(lst) - 1) for i, (o, l, r) in enumerate(lst)]
+
+    def iota(out, pat, base, cm=0):
+        def emit():
+            if SCRATCH[out["acc"][0][0]][2] == I32:
+                return g.iota(out["ap"], pat, base, cm)
+            return g.iota(out["ap"], pat, base, cm, allow_small_or_imprecise_dtypes=True)
+        return node("G", 160 + 2 * out["n"], emit, [], [out])
+
+    def fill(out, v):
+        return iota(out, [[0, out["n"]]], v)
+
+    def dma(out, a, sem, cost, cnt=16):
+        rd = [a] if isinstance(a, dict) else []
+        wr = [out] if isinstance(out, dict) else []
+        return node("S", cost, lambda: g.sync.dma_start(ap(out), ap(a)).then_inc(T.sem[sem], 16), rd, wr, sem=sem, cnt=cnt)
+
+    def ways(src):
+        used, res = 0, {}
+        for m in sorted({topo.mask(src, c) for c in T.cores if c != src}, key=lambda x: bin(x).count("1")):
+            for c in T.cores:
+                if c != src and topo.mask(src, c) == m:
+                    res[c] = m & ~used
+            used |= m
+        return res
+
+    def send(src, dst_of, arr, out, landing, cost):
+        me = T.cores[rank]
+        mine = ways(me)
+        tf = []
+        for mk in sorted(set(mine.values())):
+            qs = [q for q in range(NR) if mine.get(T.cores[q]) == mk]
+            tf.append(RemoteDMATransfer(dst_ids=[DstId(rid=topo.addr(T.cores[q])[0], pnc=topo.addr(T.cores[q])[1]) for q in qs],
+                                        dma_engine_mask=mk, remote_sem=T.sem[arr], src=src["ap"], dsts=[dst_of(q) for q in qs]))
+        sent = sum(bin(mk).count("1") for mk in set(mine.values()))
+        k = node("G", 300, lambda: g.remote_dma_fused(tf, local_sem=T.sem[out]), [src], [], sem=out, cnt=sent)
+        got = sum(bin(ways(c)[me]).count("1") for c in T.cores if c != me)
+        node("X", cost, None, [], [landing], sem=arr, cnt=got, after=[k])
+
+    dma(D("WIN", OWN, G), T.x[:, 0:G], "d0", 2200)
+    dma(C("REQ", 0, 18), T.req[:], "d1", 2200)
+    dma(A("NB"), T.nb[:], "d2", 5500)
+    dma(C("WIN", OWN + G, OWN + V), T.x[:, G:V], "d3", 6500)
+    dma(C("TH", 0, 1), T.th[:], "d4", 6500)
+    dma(A("PT"), T.pt[:], "d5", 9000)
+    iota(C("PB", 4), [[0, 1]], 0, 1)
+    iota(A("JF"), [[1, 256]], 0)
+    iota(A("DM"), [[1, 128]], 0, -1)
+    iota(A("THR"), [[128, 2], [0, 8]], -128, 1)
+    send(D("WIN", OWN, G), lambda q: T.WIN[:, GH + ((q - rank) % NR - 1) * G:GH + ((q - rank) % NR) * G],
+         "arr0", "out0", C("WIN", GH, GR), 5000)
+    iota(A("KT"), [[0, 8], [64, 16], [0, 2]], 0)
+    fill(A("X0"), 0)
+    iota(A("HI5"), [[512, 8], [0, 2]], 0)
+    iota(A("RMAX"), [[0, 16], [300, 16]], 0)
+    for n_ in ("ZZ", "PR", "OH0", "PS", "X1", "OH1"):
+        fill(A(n_), 0)
+    iota(A("DI"), [[0, 16], [1, 8]], 8)
+    iota(A("JI"), [[0, 8], [1, 16]], -16)
+    iota(C("X3", 0, 64), [[16, 8], [1, 8]], 0, -1)
+    iota(A("ZO"), [[0, 128], [0, 16]], 0)
+    ms(C("WIN", 0, 16), 0.0)
+    ms(C("WIN", 2048, OWN), 0.0)
+    dma(D("WIN", PL0, V), T.plans[:], "d6", 11000)
+    for q in range(NR):
+        d = (rank - q) % NR
+        dma(D("WIN", GR + q * G, G), D("WIN", GH + (d - 1) * G if d else OWN, G), "d7", 2000, 16 * NR)
+
+    pi = C("PB", 4)
+    ts(C("PB", 0), pi, 15, OP.bitwise_and)
+    ts(C("PB", 1), pi, 4, OP.logical_shift_right)
+    ts(C("PB", 2), pi, 4, OP.logical_shift_right, 1, OP.bitwise_and)
+    ts(C("PB", 3), pi, 3, OP.logical_shift_right, 1, OP.bitwise_and)
+    cp(C("PF", 0, 4), C("PB", 0, 4))
+    cF, gF, gbF, x3F, ngbF, qbF, lowF = (C("PF", i) for i in range(7))
+    ts(ngbF, gbF, -1.0, OP.mult, 1.0, OP.add)
+    ts(qbF, cF, -1.0 / 16, OP.mult, (15 * 4096 + 2048) / 65536, OP.add)
+    ts(C("PF", 7), gbF, 16.0, OP.mult, cF, OP.add)
+    ts(lowF, C("PF", 7), 2.0, OP.mult, 0.5, OP.add)
+    ms(C("RI", 0, 32), V)
+    cp(C("RI", 0, 5), C("REQ", 0, 5))
+    cp(C("RI", 16, 20), C("REQ", 5, 9))
+    ms(C("QL", 8, 16), 0)
+    cp(C("QL", 0, 5), C("REQ", 0, 5))
+    cp(C("QL", 8, 12), C("REQ", 5, 9))
+    ts(C("RI", 8, 16), C("RI", 0, 8), 4, OP.logical_shift_right)
+    ts(C("RI", 24, 32), C("RI", 16, 24), 4, OP.logical_shift_right)
+    cp(C("BL", 0, 32), C("RI", 0, 32))
+    cp(C("BL", 160, 168), C("REQ", 9, 17))
+    ts(C("RI", 40, 48), C("REQ", 9, 17), 4, OP.logical_shift_right)
+    cp(C("BL", 168, 176), C("RI", 40, 48))
+    cp(C("RI", 48), C("REQ", 17))
+    cp(C("QL", 80, 89), C("REQ", 9, 18))
+    ts(A("I1"), A("DM"), 0.0, OP.is_equal)
+    ts(A("IK"), A("I1"), 1024.0, OP.mult)
+    ts(A("I21"), A("I1"), 2.0 ** 21, OP.mult)
+    ts(A("IH"), A("I1"), HUGE, OP.mult, HUGE, OP.mult)
+    ts(A("LOW"), A("KT"), lowF, OP.add)
+    for u in range(2):
+        for w in range(2):
+            ts(A("SW", 2 * u + w), A("DM"), 16.0 * (w - u), OP.is_equal, gbF if u else ngbF, OP.mult)
+    ts(A("THC"), C("TH", 0), -1024.0, OP.mult, -1023.75, OP.add)
+    ms(A("RMIN"), 0.0)
+    ms(C("RMIN", 0, 256, 16), 2.0 ** 30)
+    ms(A("MI"), 0)
+    ms(A("I3"), 0)
+    ts(A("MKD"), C("JF", 0, 16), -8.0, OP.add, cF, OP.is_equal)
+    ts(A("SELD"), C("X3", 0, 64), 0.0, OP.is_equal)
+    ts(A("IA"), C("JF", 0, 240), 1.0, OP.add)
+    ts(A("MK"), C("JF", 0, 16), cF, OP.is_equal)
+    act(C("TS", 0, 16), A("THR"), AF.Exp, scale=-0.875 * float(np.log(2.0)), extra=1600)
+    for b in range(16):
+        if b % 8 < 5:
+            act(C("XT", b, W, 16), A("IA"), AF.Identity, scale=C("MK", b))
+        else:
+            ts(C("XT", b, W, 16), A("IA"), C("MK", b), OP.mult)
+    ts(C("EE", 0, 32, 2), A("MK"), BAN, OP.mult)
+    ts(C("EE", 1, 32, 2), A("MK"), 2 * BAN, OP.mult)
+    ts(C("SELF", 0, 8), C("JF", 0, 8), gF, OP.is_equal)
+    ts(C("SELF", 8, 16), C("SELF", 0, 8), cF, OP.mult)
+    ts(A("SELP"), C("SELF", 0, 8), 1 / BAN, OP.mult)
+    ts(A("SELC"), C("SELF", 8, 16), 1 / BAN, OP.mult)
+    cp(A("WF"), C("TS", 0, 16))
+    ts(A("W25"), A("WF"), 2.5, OP.mult)
+    rec(C("WI", 0, 16), A("WF"))
+    act(C("WI", 16, 32), C("WI", 0, 16), AF.Copy)
+    act(C("WI", 32, 64), C("WI", 0, 32), AF.Copy)
+    ms(A("ONE"), 1.0)
+    ms(A("R8"), 1.0)
+    ms(C("R8", 0, 128, 8), 0.0)
+    ts(C("TW", 128, 240), C("ONE", 0, 112), HUGE, OP.mult, HUGE, OP.mult)
+    ms(C("LV", 0, 16), 1.0)
+    act(A("IF"), A("I1"), AF.Copy)
+    ts(A("TRI"), A("DM"), 0.0, OP.is_gt)
+    ts(A("N01"), A("I1"), -16.0, OP.mult)
+    tt(A("TRI"), A("TRI"), A("N01"), OP.add)
+    cp(A("L16"), C("JF", 0, 64))
+    ts(A("L8"), C("JF", 0, 8), 2.0, OP.mult, x3F, OP.add)
+    ts(A("LK"), C("JF", 0, 4), 0.0, OP.mult, cF, OP.add)
+    act(A("KB"), C("JF", 0, 128), AF.Identity, bias=cF, scale=16.0)
+    ts(A("KM"), C("KB", 0, 16), float(GR + rank * G), OP.add)
+    ts(A("K0"), A("KB"), float(OWN), OP.add)
+    ts(A("K1"), A("KB"), float(TB1), OP.add)
+
+    def halves(H):
+        return [(0, 16)] if H == 8 else [(0, H), (8, 8 + H)]
+
+    def comers(r, k):
+        H = 8 if r else 5
+        s = (r * 5 + k) * 32
+        X = "X%d" % (k % 2)
+        for l in range(2):
+            act(D(X, l * 128, 16 * H), IND(A("XT"), D("BL", s + 16 * l, H)), AF.Copy)
+        lst = []
+        for l in range(2):
+            lst += grp([(D("F1", 256 + l * 16, 16), D(X, l * 128, 128), A("SELF"))])
+            if k < 4:
+                lst += grp([(D("F1", l * 128, 128), D(X, l * 128, 128), A("I1"))])
+        mm(lst)
+        act(A("FH", k), C("F1", 256, 288), AF.Copy)
+        if k < 4:
+            for l in range(2):
+                ts(D("ZW", k * 256 + l * 128, 128), D("F1", l * 128, 128), 1.0, OP.min, C("WF", l * 8), OP.mult)
+
+    def conflicts(r, k):
+        H = 8 if r else 5
+        s = (r * 5 + k) * 32
+        X = "X%d" % (k % 2)
+        fm = D("FM", k * 16, 16)
+        tt(fm, A("FH", k, ALL, 0), D("LV", k * 16, 16), OP.mult)
+        if k == 4:
+            return
+        tt(A("THR"), fm, A("W25"), OP.mult)
+        for c in range(16):
+            ts(D("OA", (k * 16 + c) * 128, 128), C("IA", 0, 128), C("FM", k * 16 + c), OP.is_equal)
+        last = mm([(C("TT", 0, 128), A("IH"), A("M01" if r or k else "ZZ"), True, False)])
+        for h in range(2):
+            last = mm([(D("TT", gg * 16, 16), D("OA", (k * 16 + h * 8 + gg) * 128, 128), D("ZW", k * 256 + h * 128 + gg * 16, 16),
+                        False, h == 1 and gg == 7) for gg in range(8)], after=[last])
+        act(A("TS"), C("TT", 0, 128), AF.Copy)
+        mm(grp([(C("TM", 0, 128), A("TS"), A("I1"))]))
+        act(C("TW", 0, 128), C("TM", 0, 128), AF.Copy)
+        if k < 3:
+            act(A("M01"), A("TS"), AF.Sign)
+        for l in range(2):
+            tt(D("PR", l * 128, 16 * H), IND(A("TW"), D("BL", s + 16 * l + 8, H)), D(X, l * 128, 16 * H), OP.mult)
+        mm(grp([(C("SM", 0, 8), C("PR", 0, 128), C("SELF", 0, 8))]) + grp([(C("SM", 8, 16), C("PR", 128, 256), C("SELF", 0, 8))]))
+        tt(D("RE", k * 16, 16), C("SM", 0, 16), A("THR"), OP.is_lt)
+
+    def step(r, k):
+        H = 8 if r else 5
+        n = 32 * H
+        s = (r * 5 + k) * 32
+        sq = (r * 5 + k) * 16
+        e = str(k % 2)
+        Q, PX, P, T2, OL, OH = "Q" + e, "PX" + e, "P" + e, "T" + e, "OL" + e, "OH" + e
+        OHP = "OH%d" % ((k + 1) % 2)
+        tab = D("WIN", TB1 if r else OWN, W)
+        if r and not k:
+            act(A("OB"), IND(A("EE"), C("CL", 0, 7)), AF.Copy)
+        for bi, (h0, h1) in enumerate(BLOCKS[r]):
+            S, m = "S%d" % bi, 32 * (h1 - h0)
+            for l in range(2):
+                cp(C(Q, h0 * 32 + l, h1 * 32, 2), IND(A("NB"), C("QL", sq + 8 * l + h0, sq + 8 * l + h1)))
+            last = mm([(C(S, 0, m), A("I1"), C("LOW", 0, m), True, False)])
+            for h in range(h0, h1):
+                gather("V" if h in DVE_CHUNKS.get((r, k), ()) else "A", D(P, h * 512, 512), IND(tab, D(Q, h * 32, 32)),
+                       after=sgs[-1:] if h == h0 + 1 else ())
+                tr(D(T2, h * 512, 512), D(P, h * 512, 512))
+                if h % 2 or h == h1 - 1:
+                    u = h - h % 2
+                    last = mm([(C(S, (u - h0) * 32, (h + 1 - h0) * 32), A("IK"), C(P, u * 512 + i, h * 512 + 512, 16), False,
+                                not (r or k) and h == h1 - 1 and i == 15) for i in range(16)], after=[last])
+            if k:
+                mm([(C(S, l, m, 2), A("SW", 2 * l + gb), C(OHP, gb * 128 + h0 * 16, gb * 128 + h1 * 16), False, l + gb == 2)
+                    for l in range(2) for gb in range(2)], after=[last])
+            elif r:
+                u = max(h0, 1)
+                mm([(C(S, (u - h0) * 32 + 1, m, 2), A("I1"), C("OB", (u - 1) * 16, (h1 - 1) * 16), False, True)], after=[last])
+            sg = C("SG", h0 * 32, h1 * 32)
+            act(sg, C(S, 0, m), AF.Sign, bias=A("THC"))
+            sgs.append(act(C("SU", h0 * 32, h1 * 32), sg, AF.Identity, scale=2.0 ** 21 + 0.5))
+        ts(C("QF", 0, n), C(Q, 0, n), -2048.0, OP.add)
+        lst = []
+        for gb in range(2):
+            lst += grp([(A("QQ", slice(0, H), gb), A("SW", 2 * gb + l), C("QF", l, n, 2)) for l in range(2)])
+        mm(lst)
+        act(C("QS", 0, n), A("QQ", slice(0, H)), AF.Identity, bias=qbF, scale=1 / 65536)
+        for a, b in halves(H):
+            ts(C(PX, a * 16, b * 16), IND(A("PT"), C("QL", sq + a, sq + b)), 4194304.0, OP.add)
+        for l in range(2):
+            ts(C("CST", l, n, 2), D(PX, l * 128, 16 * H), 1, OP.logical_shift_right, 1023 << 10, OP.bitwise_and)
+        for bi, (h0, h1) in enumerate(BLOCKS[r]):
+            S, m, a, b = "S%d" % bi, 32 * (h1 - h0), 32 * h0, 32 * h1
+            tt(D(S, 256, m), C(S, 0, m), C("CST", a, b), OP.add)
+            for l in range(2):
+                tt(A("KEY", slice(h0, h1), l), C(S, 256 + l, 256 + m, 2), C("SU", a + l, b, 2), OP.add)
+            tr(C("KT", a, b), A("KEY", slice(h0, h1)))
+            scan(C("SC", a, b), C("RMIN", 0, m), C("KT", a, b), OP.add, OP.min)
+            mi, i2 = C("MI", 2 * h0, 2 * h1), C("I2", 2 * h0, 2 * h1)
+            cp(mi, C("SC", a + 15, b, 16))
+            ts(i2, mi, 1, OP.logical_shift_right, 511, OP.bitwise_and)
+            tt(i2, i2, C("HI5", 0, 2 * (h1 - h0)), OP.add)
+            cp(C(OL, 2 * h0, 2 * h1), i2)
+            tt(C("K2", a, b), IND(C(T2, a * 16, b * 16), C(OL, 2 * h0, 2 * h1)), C("QS", a, b), OP.add)
+            tr(C("K2T", a, b), C("K2", a, b))
+            scan(C("SC2", a, b), C("RMAX", 0, m), C("K2T", a, b), OP.min, OP.max)
+            ts(C("BI", 2 * h0, 2 * h1), C("SC2", a + 15, b, 16), 65536.0, OP.mult)
+            if (r, k) != (1, 3):
+                ts(C("I3", 2 * h0, 2 * h1), C("BI", 2 * h0, 2 * h1), 4095, OP.bitwise_and)
+            if k < 3:
+                for l in range(2):
+                    ts(C("QL", sq + 16 + 8 * l + h0, sq + 16 + 8 * l + h1), C("I3", 2 * h0 + l, 2 * h1, 2), V - 1.0, OP.min)
+        ts(D("I3", 16, 2 * H), C("BI", 0, 2 * H), 4 if k < 3 else 8, OP.logical_shift_right, 255 if k < 3 else 15, OP.bitwise_and)
+        for l in range(2):
+            cp(D("BL", s + 32 + 16 * l, 16), C("I3", l, 32, 2))
+        ts(C("I2", 16, 32), A("MI"), 31, OP.bitwise_and)
+        for gb in range(2):
+            cp(D(OL, 16 + 8 * gb, 8), C("I2", 16 + gb, 32, 2))
+        for a, b in halves(H):
+            act(C(OH, a * 16, b * 16), IND(A("EE"), C(OL, 16 + a, 16 + b)), AF.Copy)
+        lst = []
+        for l in range(2):
+            lst += grp([(D("OC", l * 128, 16 * H), A("SW", 2 * l + gb), D(OH, gb * 128, 16 * H)) for gb in range(2)])
+        mm(lst)
+        for a, b in halves(H):
+            tt(C("PS", a * 16, b * 16), C("OC", a * 16, b * 16), C(PX, a * 16, b * 16), OP.mult)
+        lst = []
+        for l in range(2):
+            lst += grp([(D("OC", 256 + l * 16, 8), D("PS", l * 128, 128), A("SELP"))])
+            for gb in range(2):
+                lst += grp([(C("OC", 264 + l * 16 + gb, 272 + l * 16, 2), D(OH, gb * 128, 128), C("SELC", l, 8, 2))])
+        mm(lst)
+        act(A("PH", k), C("OC", 256, 288), AF.Copy)
+        ts(D("OV", k * 16, 16), A("PH", k, ALL, 0), 8388608.0, OP.is_ge)
+
+    def table():
+        tt(A("VAL"), IND(A("GO"), A("LK")), A("PLW"), OP.mult)
+        for k in range(4):
+            tt(D("ZV", k * 256, 256), IND(A("VAL"), D("L16", k * 16, 16)), D("ZW", k * 256, 256), OP.mult)
+        last = mm([(C("TT", 0, 128), A("I1"), A("ZZ"), True, False)])
+        for k in range(4):
+            last = mm([(D("TT", gg * 16, 16), D("OA", (k * 16 + l * 8 + gg) * 128, 128), D("ZV", k * 256 + l * 128 + gg * 16, 16),
+                        False, k == 3 and l == 1 and gg == 7) for gg in range(8) for l in range(2)], after=[last])
+        act(A("PTS"), C("TT", 0, 128), AF.Copy)
+        act(A("N01"), C("TT", 0, 128), AF.Relu, bias=C("LV", 0), scale=-1.0)
+        mm(grp([(C("TM", 0, 128), A("PTS"), A("IF")), (C("TM", 0, 128), A("N01"), A("I21"))]))
+
+    def index(out, a, b, keep):
+        tt(C("X3", a, b), C("TM", a, b), keep, OP.min)
+        cp(out, C("X3", a, b))
+
+    def finish(r):
+        H = 8 if r else 5
+        s = (r * 5 + 4) * 32 + 8
+        act(A("E1"), A("OV"), AF.Identity, bias=C("LV", 0), scale=-0.5)
+        tt(A("E2"), A("PH", ALL, ALL, 0), A("E1"), OP.mult)
+        ts(A("E3"), A("E2"), 2047, OP.bitwise_and)
+        ts(A("E1"), A("E3"), 1.0, OP.add)
+        tt(A("PLW"), A("E1"), A("RE"), OP.mult)
+        tt(A("PLW"), A("PLW"), A("WI"), OP.mult)
+        tt(A("GD"), A("RE"), C("LV", 16, 80), OP.subtract)
+        tt(C("GD", 0, 32), C("GD", 0, 32), C("GD", 32, 64), OP.add)
+        tt(C("GD", 0, 16), C("GD", 0, 16), C("GD", 16, 32), OP.add)
+        tt(C("AM", 16, 32), C("FM", 16, 32), C("FM", 32, 48), OP.max)
+        tt(C("AM", 32, 48), C("AM", 16, 32), C("FM", 48, 64), OP.max)
+        ts(C("DD", 16, 32), C("AM", 32, 48), -1.0, OP.add)
+        ts(C("DD", 0, 16), C("DD", 16, 32), 4, OP.arith_shift_right)
+        tt(A("INP"), IND(C("DD", 0, 16), A("L8")), A("DI"), OP.is_equal)
+        act(A("LVB"), IND(C("LV", 64, 80), A("L8")), AF.Copy)
+        for l in range(2):
+            gather("AV"[l], D("PR", l * 128, 16 * H), IND(A("MKD"), D("BL", s + 16 * l, H)))
+        last = mm([(C("S1", 0, 128), A("I1"), A(n_), i == 0, False) for i, n_ in enumerate(("INP", "INP", "LVB"))])
+        mm([(D("S1", 64 * l, 64), D("PR", l * 128, 128), A("SELD"), False, l == 1) for l in range(2)], after=[last])
+        ts(A("IND"), C("S1", 0, 128), 2.0, OP.is_ge)
+        mm(grp([(C("S0", 0, 64), A("TRI"), C("IND", 0, 64))]) +
+           grp([(C("S0", 64, 128), A("ONE"), C("IND", 0, 64)), (C("S0", 64, 128), A("TRI"), C("IND", 64, 128))]))
+        tt(A("CI"), C("S0", 0, 128), A("IND"), OP.mult)
+        scan(A("RK"), A("R8"), A("CI"), OP.mult, OP.add)
+        tt(A("GO"), C("RK", 7, 128, 8), C("GD", 0, 16), OP.is_lt)
+        table()
+        if r:
+            for h in range(2):
+                index(D("IX", h * 64, 64), h * 64, h * 64 + 64, D("K1", h * 64, 64))
+            for c in range(8):
+                gather("AVAVAVAV"[c], D("Y", c * G, G), IND(C("WIN", 0, TB1 + V), D("IX", c * 16, 16)))
+            for c in range(4):
+                dma(T.y[:, c * 512:c * 512 + 512], D("Y", c * 512, 512), "d%d" % (8 + c), 2000)
+            return
+        am = C("AM", 0, 16)
+        tt(am, C("AM", 32, 48), C("FM", 64, 80), OP.max)
+        ts(C("DD", 16, 32), am, -1.0, OP.add)
+        ts(A("OO"), C("FM", 16, 80), 128.0, OP.is_gt)
+        tt(A("OS", 0), A("OO"), A("FH", slice(1, 5), ALL, 1), OP.mult)
+        tt(A("OS", 1), A("OO"), A("PH", ALL, ALL, 1), OP.mult)
+        tt(A("O2"), A("OS", ALL, slice(0, 2)), A("OS", ALL, slice(2, 4)), OP.add)
+        tt(C("O4", 0, 16), C("O2", 0, 16), C("O2", 16, 32), OP.add)
+        tt(C("PAY", 16, 32), C("O2", 32, 48), C("O2", 48, 64), OP.add)
+        ts(C("O4", 16, 32), am, 1.0, OP.max)
+        rec(C("OO", 0, 16), C("O4", 16, 32))
+        tt(C("O4", 16, 32), C("O4", 0, 16), C("OO", 0, 16), OP.mult)
+        cp(C("O3", 0, 16), C("O4", 16, 32))
+        ts(C("O3", 16, 32), C("DD", 16, 32), 15, OP.bitwise_and)
+        ts(C("O4", 32, 48), C("O3", 16, 32), 16.0, OP.mult, 1.0, OP.add)
+        tt(C("PAY", 0, 16), C("O4", 32, 48), C("O3", 0, 16), OP.add)
+        for f in range(2):
+            tt(C("PIB", f, 256, 2), IND(D("PAY", f * 16, 16), A("L8")), A("IND"), OP.mult)
+        act(A("RKC"), C("RK", 7, 128, 8), AF.Copy)
+        for l in range(2):
+            tt(D("SG", 128 * l, 128), IND(A("RKC"), D("L16", 8 * l, 8)), A("JI"), OP.is_equal)
+            act(A("ZO", slice(64 * l, 64 * l + 64, 9)), D("SG", 128 * l, 128), AF.Copy)
+        mm(grp([(C("SM", 32, 48), A("ZO", slice(c * 8, c * 8 + 8)), D("PIB", c * 16, 16)) for c in range(16)]))
+        ts(C("O4", 0, 8), C("SM", 32, 48, 2), 0.0, OP.is_equal, 2049.0, OP.mult)
+        tt(C("O4", 8, 16), C("SM", 32, 48, 2), C("O4", 0, 8), OP.add)
+        ts(C("MSG", 16, 24), C("O4", 8, 16), -1.0, OP.add)
+        cp(C("MSG", 24, 32), C("SM", 33, 48, 2))
+        index(C("MSG", 0, 16), 0, 16, A("KM"))
+        send(A("MSG"), lambda q: T.LAND[:, ((rank - q) % NR - 1) * 32:((rank - q) % NR) * 32], "arr1", "out1", A("LAND"), 5000)
+        index(A("IX"), 0, 128, A("K0"))
+        for c in range(8):
+            gather("AVAVAAVA"[c], D("WIN", TB1 + c * G, G), IND(C("WIN", 0, TB1), D("IX", c * 16, 16)))
+        tt(A("FZ"), C("RE", 0, 16), A("GO"), OP.is_gt)
+        tt(A("ZF"), IND(A("FZ"), C("L16", 0, 16)), C("ZW", 0, 256), OP.mult)
+        lst = []
+        for gg in range(8):
+            lst += grp([(D("TT", gg * 16, 16), D("OA", (l * 8 + gg) * 128, 128), D("ZF", l * 128 + gg * 16, 16)) for l in range(2)])
+        mm(lst)
+        act(A("M01"), C("TT", 0, 128), AF.Sign)
+        ts(C("QL", 89, 96), C("LAND", 16, 224, 33), V - 1.0, OP.min)
+        cp(C("CL", 0, 7), C("LAND", 24, 224, 33))
+        cp(C("RI", 49, 56), C("LAND", 16, 224, 33))
+        ts(C("RI", 56, 64), C("RI", 48, 56), 4, OP.logical_shift_right)
+        cp(C("BL", 176, 192), C("RI", 48, 64))
+        for d in range(1, NR):
+            gather("VA"[d % 2], D("WIN", TB1 + V + (NR - d - 1) * G, G), IND(C("WIN", 0, TB1), D("LAND", (d - 1) * 32, 16)))
+
+    for r in range(2):
+        for k in range(4):
+            comers(r, k)
+            conflicts(r, k)
+            step(r, k)
+            tt(D("LV", k * 16 + 16, 16), D("RE", k * 16, 16), D("OV", k * 16, 16), OP.mult)
+        if not r:
+            comers(r, 4)
+            conflicts(r, 4)
+        finish(r)
+    return nodes
+
+
+def schedule(nodes, bias, lat_x, lat_s, cost):
+    n = len(nodes)
+    eng = [nd["eng"] for nd in nodes]
+    succ = [[] for _ in range(n)]
+    for k, nd in enumerate(nodes):
+        for j, hard in nd["deps"].items():
+            succ[j].append((k, (lat_s if eng[j] == eng[k] else lat_x) if hard else 0))
+    pr = [0.0] * n
+    for k in range(n - 1, -1, -1):
+        pr[k] = cost[k] + max([pr[s] + la for s, la in succ[k]], default=0)
+    pr = [pr[k] + bias[k] for k in range(n)]
+    left = [len(nd["deps"]) for nd in nodes]
+    ready_at = [0.0] * n
+    end = [0.0] * n
+    free = {e: 0.0 for e in "VAPGSX"}
+    pool = {e: [k for k in range(n) if eng[k] == e and not left[k]] for e in "VAPGSX"}
+    order = {e: [] for e in "VAPGSX"}
+    queued = {e: [k for k in range(n) if eng[k] == e] for e in "GSX"}
+    for _ in range(n):
+        best = None
+        for e in "VAPGSX":
+            if pool[e]:
+                if e in "GSX":
+                    k = queued[e][len(order[e])]
+                    if k not in pool[e]:
+                        continue
+                    t = max(free[e], ready_at[k])
+                else:
+                    t = max(free[e], min(ready_at[k] for k in pool[e]))
+                    k = max((k for k in pool[e] if ready_at[k] <= t + SLACK), key=lambda k: pr[k])
+                    t = max(t, ready_at[k])
+                if best is None or t < best[0]:
+                    best = (t, e, k)
+        t, e, k = best
+        pool[e].remove(k)
+        order[e].append(k)
+        end[k] = t + cost[k]
+        free[e] = t + (60 if e in "SX" else cost[k])
+        for s, la in succ[k]:
+            ready_at[s] = max(ready_at[s], end[k] + la)
+            left[s] -= 1
+            if not left[s]:
+                pool[eng[s]].append(s)
+    return order, end
+
+
+def replay(nodes, order, lat_x, lat_s, cost):
+    end = {}
+    pos = {e: 0 for e in order}
+    free = {e: 0.0 for e in order}
+    while len(end) < len(nodes):
+        for e in order:
+            while pos[e] < len(order[e]):
+                k = order[e][pos[e]]
+                deps = nodes[k]["deps"]
+                if any(j not in end for j in deps):
+                    break
+                t = max([free[e]] + [end[j] + ((lat_s if nodes[j]["eng"] == e else lat_x) if h else 0) for j, h in deps.items()])
+                end[k] = t + cost[k]
+                free[e] = t + (60 if e in "SX" else cost[k])
+                pos[e] += 1
+    return max(end.values())
+
+
+def tuned(nodes):
+    n = len(nodes)
+    c1 = [nd["cost"] for nd in nodes]
+    c2 = [nd["cost"] * (1.5 if nd["eng"] == "P" else 1) + (30 if nd["eng"] in "VA" else 0) for nd in nodes]
+
+    def value(b):
+        o, e = schedule(nodes, b, 150, 100, c1)
+        return max(e) + replay(nodes, o, 250, 150, c2), o
+    rng = np.random.default_rng(0)
+    bias = np.zeros(n)
+    best = value(bias)
+    for _ in range(TRIES):
+        c = bias.copy()
+        i = int(rng.integers(n))
+        d = rng.normal() * 1500
+        if rng.integers(2):
+            c[i:i + int(rng.integers(1, 40))] += d
+        else:
+            for k in range(max(0, i - 60), min(n, i + 60)):
+                if nodes[k]["lab"] == nodes[i]["lab"]:
+                    c[k] += d
+        v = value(c)
+        if v[0] <= best[0]:
+            best, bias = v, c
+    return best[1]
+
+
+def rank_program(g, core, T, topo):
+    rank = T.rank_of(core)
+    if rank is None:
+        return
+    nodes = build(g, T, rank, topo)
+    if "o" not in ORDER:
+        ORDER["o"] = tuned(nodes)
+    order = ORDER["o"]
+    queue = {"V": g.vector, "A": g.scalar, "P": g.tensor, "G": g, "S": g.sync}
+    own = {"V": "sv", "A": "sa", "P": "sp", "G": "sg"}
+    needed = set()
+    for nd in nodes:
+        if nd["eng"] != "X":
+            needed.update(j for j, hard in nd["deps"].items() if hard)
+    mark = {}
+    total = {}
+    for e in "VAPG":
+        for k in order[e]:
+            if nodes[k]["sem"] is None and k in needed:
+                total[own[e]] = total.get(own[e], 0) + 1
+                mark[k] = (own[e], total[own[e]])
+    for k, nd in enumerate(nodes):
+        if nd["sem"] is not None:
+            mark[k] = (nd["sem"], nd["cnt"])
+            total[nd["sem"]] = nd["cnt"]
+    for e in "SGVAP":
+        seen = {}
+        for k in order[e]:
+            want = {}
+            for j, hard in nodes[k]["deps"].items():
+                if hard:
+                    want[mark[j][0]] = max(want.get(mark[j][0], 0), mark[j][1])
+            for s, c in want.items():
+                if seen.get(s, 0) < c:
+                    queue[e].wait_ge(T.sem[s], c)
+                    seen[s] = c
+            ins = nodes[k]["emit"]()
+            if nodes[k]["sem"] is None and k in mark:
+                ins.then_inc(T.sem[mark[k][0]], 1)
+        if e == "S":
+            for s, c in total.items():
+                if seen.get(s, 0) < c:
+                    g.sync.wait_ge(T.sem[s], c)

@@ -9,17 +9,17 @@ F32, BF, F16, I32, U16 = "float32", "bfloat16", "float16", "int32", "uint16"
 SMALL = {"MK": 16, "WF": 16, "W25": 16, "WI": 64, "KM": 16, "FM": 80, "THR": 16, "RE": 64, "LV": 80, "OV": 64, "E1": 64,
          "PLW": 64, "GD": 64, "AM": 48, "GO": 16, "VAL": 64, "FZ": 16, "OO": 64, "O2": 64, "RKC": 16, "PAY": 32, "O4": 48}
 BUFS = {
-    I32: {"NB": V, "PT": V, "REQ": 32, "TH": 4, "PB": 8, "HI5": 16, "RI": 64, "PX0": 256, "PX1": 256, "CST": 256, "MI": 16,
+    I32: {"NB": V, "PT": V, "REQ": 32, "TH": 4, "PB": 8, "RI": 64, "PX0": 256, "PX1": 256, "CST": 256, "MI": 16,
           "I2": 32, "BI": 16, "I3": 32, "E2": 64, "E3": 64, "DD": 32, "O3": 32},
     BF: {"WIN": WEND, "Y": V, "XT": W, "I1": 128, "IK": 128, "IH": 128, "SW": (4, 128), "I21": 128, "SELD": 64,
-         "MKD": 16, "TRI": 128, "ONE": 128, "SELF": 16, "SELC": 8, "RMIN": 256, "EE": 32, "IA": 240, "P0": 4096, "P1": 4096,
+         "MKD": 16, "TRI": 128, "ONE": 128, "SELF": 16, "SELC": 8, "RMIN": 128, "EE": 32, "IA": 240, "P0": 4096, "P1": 4096,
          "T0": 4096, "T1": 4096, "SG": 256, "OH0": 256, "OH1": 256, "OB": 112, "X0": 256, "X1": 256, "ZW": 1024, "OA": 8192,
          "ZF": 256, "TS": 128, "TW": 240, "M01": 128, "PR": 256, "IND": 128, "LVB": 128, "INP": 128, "N01": 128,
          "ZO": (128, 16), "ZZ": 128, "PIB": 256},
     U16: {"LAND": 224, "MSG": 32, "L16": 64, "L8": 8, "LK": 4, "BL": 320, "QL": 160, "Q0": 256, "Q1": 256, "OL0": 32,
           "OL1": 32, "CL": 8, "IX": 128},
-    F16: {"LOW": 256, "QF": 256, "ZV": 1024},
-    F32: {"SF": sum(SMALL.values()), "PF": 8, "DM": 128, "JF": 256, "IF": 128, "SELP": 8, "RMAX": 256, "R8": 128, "DI": 128,
+    F16: {"LOW": 128, "QF": 256, "ZV": 1024},
+    F32: {"SF": sum(SMALL.values()), "PF": 8, "DM": 128, "JF": 256, "IF": 128, "SELP": 8, "RMAX": 128, "R8": 128, "DI": 128,
           "JI": 128, "KB": 128, "K0": 128, "K1": 128, "THC": 1, "QS": 256, "SU": 256, "KEY": (8, 2, 16), "KT": 256, "SC": 256,
           "K2": 256, "K2T": 256, "SC2": 256, "PS": 256, "FH": (5, 2, 2, 8), "PH": (4, 2, 2, 8), "CI": 128, "RK": 128,
           "PTS": 128, "X3": 128, "OS": (2, 4, 16)},
@@ -30,9 +30,9 @@ SCRATCH["QQ"] = ("psum", [128, 16, 2, 16], F32)
 SEMAPHORES = ["sv", "sa", "sp", "sg", "arr0", "arr1", "out0", "out1"] + ["d%d" % i for i in range(12)]
 HUGE = 2.0 ** 58
 BAN = 2.0 ** 24
-PE_CYC, SLACK, TRIES = 0.5, 40, 1200
+PE_CYC, SLACK, TRIES = 0.5, 80, 1200
 BLOCKS = (((0, 2), (2, 5)), ((0, 4), (4, 8)))
-DVE_CHUNKS = {(0, 0): (1,), (1, 0): (1, 3)}
+DVE_CHUNKS = {(0, 0): (1, 3), (1, 0): (1, 3)}
 ORDER = {}
 
 
@@ -155,17 +155,20 @@ def build(g, T, rank, topo):
     def fill(out, v):
         return iota(out, [[0, out["n"]]], v)
 
-    def dma(out, a, sem, cost, cnt=16):
-        rd = [a] if isinstance(a, dict) else []
+    def dma(out, a, sem, cost, cnt=16, behind=None):
         wr = [out] if isinstance(out, dict) else []
-        return node("S", cost, lambda: g.sync.dma_start(ap(out), ap(a)).then_inc(T.sem[sem], 16), rd, wr, sem=sem, cnt=cnt)
+        return node("S", cost, lambda: g.sync.dma_start(ap(out), ap(a)).then_inc(T.sem[sem], 16), [a, behind], wr, sem=sem, cnt=cnt)
 
     def ways(src):
-        used, res = 0, {}
+        used, res, load = 0, {}, None
         for m in sorted({topo.mask(src, c) for c in T.cores if c != src}, key=lambda x: bin(x).count("1")):
-            for c in T.cores:
-                if c != src and topo.mask(src, c) == m:
-                    res[c] = m & ~used
+            to = [c for c in T.cores if c != src and topo.mask(src, c) == m]
+            free = [e for e in topo.engines(src, to[0]) if not used >> e & 1]
+            load = load or len(to) / len(free)
+            while len(free) > 1 and 2 * len(to) / len(free) <= load:
+                free = free[::2]
+            for c in to:
+                res[c] = sum(1 << e for e in free)
             used |= m
         return res
 
@@ -184,20 +187,19 @@ def build(g, T, rank, topo):
 
     dma(D("WIN", OWN, G), T.x[:, 0:G], "d0", 2200)
     dma(C("REQ", 0, 18), T.req[:], "d1", 2200)
-    dma(A("NB"), T.nb[:], "d2", 5500)
-    dma(C("WIN", OWN + G, OWN + V), T.x[:, G:V], "d3", 6500)
-    dma(C("TH", 0, 1), T.th[:], "d4", 6500)
-    dma(A("PT"), T.pt[:], "d5", 9000)
+    dma(A("NB"), T.nb[:], "d2", 6000)
+    dma(C("WIN", OWN + G, OWN + V), T.x[:, G:V], "d3", 7000)
+    dma(C("TH", 0, 1), T.th[:], "d4", 7000)
+    dma(A("PT"), T.pt[:], "d5", 4500, behind=A("NB"))
     iota(C("PB", 4), [[0, 1]], 0, 1)
     iota(A("JF"), [[1, 256]], 0)
     iota(A("DM"), [[1, 128]], 0, -1)
     iota(A("THR"), [[128, 2], [0, 8]], -128, 1)
     send(D("WIN", OWN, G), lambda q: T.WIN[:, GH + ((q - rank) % NR - 1) * G:GH + ((q - rank) % NR) * G],
-         "arr0", "out0", C("WIN", GH, GR), 5000)
-    iota(A("KT"), [[0, 8], [64, 16], [0, 2]], 0)
+         "arr0", "out0", C("WIN", GH, GR), 6000)
+    iota(C("KT", 0, 128), [[512, 4], [32, 16], [0, 2]], 0)
     fill(A("X0"), 0)
-    iota(A("HI5"), [[512, 8], [0, 2]], 0)
-    iota(A("RMAX"), [[0, 16], [300, 16]], 0)
+    iota(A("RMAX"), [[0, 8], [300, 16]], 0)
     for n_ in ("ZZ", "PR", "OH0", "PS", "X1", "OH1"):
         fill(A(n_), 0)
     iota(A("DI"), [[0, 16], [1, 8]], 8)
@@ -206,7 +208,7 @@ def build(g, T, rank, topo):
     iota(A("ZO"), [[0, 128], [0, 16]], 0)
     ms(C("WIN", 0, 16), 0.0)
     ms(C("WIN", 2048, OWN), 0.0)
-    dma(D("WIN", PL0, V), T.plans[:], "d6", 11000)
+    dma(D("WIN", PL0, V), T.plans[:], "d6", 3500, behind=A("PT"))
     for q in range(NR):
         d = (rank - q) % NR
         dma(D("WIN", GR + q * G, G), D("WIN", GH + (d - 1) * G if d else OWN, G), "d7", 2000, 16 * NR)
@@ -220,8 +222,8 @@ def build(g, T, rank, topo):
     cF, gF, gbF, x3F, ngbF, qbF, lowF = (C("PF", i) for i in range(7))
     ts(ngbF, gbF, -1.0, OP.mult, 1.0, OP.add)
     ts(qbF, cF, -1.0 / 16, OP.mult, (15 * 4096 + 2048) / 65536, OP.add)
-    ts(C("PF", 7), gbF, 16.0, OP.mult, cF, OP.add)
-    ts(lowF, C("PF", 7), 2.0, OP.mult, 0.5, OP.add)
+    ts(lowF, gbF, 16.0, OP.mult, cF, OP.add)
+    ms(C("PF", 7), 0.25)
     ms(C("RI", 0, 32), V)
     cp(C("RI", 0, 5), C("REQ", 0, 5))
     cp(C("RI", 16, 20), C("REQ", 5, 9))
@@ -237,16 +239,16 @@ def build(g, T, rank, topo):
     cp(C("RI", 48), C("REQ", 17))
     cp(C("QL", 80, 89), C("REQ", 9, 18))
     ts(A("I1"), A("DM"), 0.0, OP.is_equal)
-    ts(A("IK"), A("I1"), 1024.0, OP.mult)
+    ts(A("IK"), A("I1"), 2048.0, OP.mult)
     ts(A("I21"), A("I1"), 2.0 ** 21, OP.mult)
     ts(A("IH"), A("I1"), HUGE, OP.mult, HUGE, OP.mult)
-    ts(A("LOW"), A("KT"), lowF, OP.add)
+    ts(A("LOW"), C("KT", 0, 128), lowF, OP.add)
     for u in range(2):
         for w in range(2):
             ts(A("SW", 2 * u + w), A("DM"), 16.0 * (w - u), OP.is_equal, gbF if u else ngbF, OP.mult)
-    ts(A("THC"), C("TH", 0), -1024.0, OP.mult, -1023.75, OP.add)
+    ts(A("THC"), C("TH", 0), -2048.0, OP.mult, -2047.5, OP.add)
     ms(A("RMIN"), 0.0)
-    ms(C("RMIN", 0, 256, 16), 2.0 ** 30)
+    ms(C("RMIN", 0, 128, 16), 2.0 ** 30)
     ms(A("MI"), 0)
     ms(A("I3"), 0)
     ts(A("MKD"), C("JF", 0, 16), -8.0, OP.add, cF, OP.is_equal)
@@ -259,8 +261,8 @@ def build(g, T, rank, topo):
             act(C("XT", b, W, 16), A("IA"), AF.Identity, scale=C("MK", b))
         else:
             ts(C("XT", b, W, 16), A("IA"), C("MK", b), OP.mult)
-    ts(C("EE", 0, 32, 2), A("MK"), BAN, OP.mult)
-    ts(C("EE", 1, 32, 2), A("MK"), 2 * BAN, OP.mult)
+    ts(C("EE", 1, 32, 2), A("MK"), BAN, OP.mult)
+    ts(C("EE", 0, 32, 2), A("MK"), 2 * BAN, OP.mult)
     ts(C("SELF", 0, 8), C("JF", 0, 8), gF, OP.is_equal)
     ts(C("SELF", 8, 16), C("SELF", 0, 8), cF, OP.mult)
     ts(A("SELP"), C("SELF", 0, 8), 1 / BAN, OP.mult)
@@ -364,7 +366,7 @@ def build(g, T, rank, topo):
                 mm([(C(S, (u - h0) * 32 + 1, m, 2), A("I1"), C("OB", (u - 1) * 16, (h1 - 1) * 16), False, True)], after=[last])
             sg = C("SG", h0 * 32, h1 * 32)
             act(sg, C(S, 0, m), AF.Sign, bias=A("THC"))
-            sgs.append(act(C("SU", h0 * 32, h1 * 32), sg, AF.Identity, scale=2.0 ** 21 + 0.5))
+            sgs.append(act(C("SU", h0 * 32, h1 * 32), sg, AF.Identity, bias=C("PF", 7), scale=2.0 ** 22 - 0.25))
         ts(C("QF", 0, n), C(Q, 0, n), -2048.0, OP.add)
         lst = []
         for gb in range(2):
@@ -374,7 +376,7 @@ def build(g, T, rank, topo):
         for a, b in halves(H):
             ts(C(PX, a * 16, b * 16), IND(A("PT"), C("QL", sq + a, sq + b)), 4194304.0, OP.add)
         for l in range(2):
-            ts(C("CST", l, n, 2), D(PX, l * 128, 16 * H), 1, OP.logical_shift_right, 1023 << 10, OP.bitwise_and)
+            ts(C("CST", l, n, 2), D(PX, l * 128, 16 * H), 1023 << 11, OP.bitwise_and)
         for bi, (h0, h1) in enumerate(BLOCKS[r]):
             S, m, a, b = "S%d" % bi, 32 * (h1 - h0), 32 * h0, 32 * h1
             tt(D(S, 256, m), C(S, 0, m), C("CST", a, b), OP.add)
@@ -383,9 +385,8 @@ def build(g, T, rank, topo):
             tr(C("KT", a, b), A("KEY", slice(h0, h1)))
             scan(C("SC", a, b), C("RMIN", 0, m), C("KT", a, b), OP.add, OP.min)
             mi, i2 = C("MI", 2 * h0, 2 * h1), C("I2", 2 * h0, 2 * h1)
-            cp(mi, C("SC", a + 15, b, 16))
-            ts(i2, mi, 1, OP.logical_shift_right, 511, OP.bitwise_and)
-            tt(i2, i2, C("HI5", 0, 2 * (h1 - h0)), OP.add)
+            ts(mi, C("SC", a + 15, b, 16), 2.0, OP.mult)
+            ts(i2, mi, 1, OP.logical_shift_right, 2047, OP.bitwise_and)
             cp(C(OL, 2 * h0, 2 * h1), i2)
             tt(C("K2", a, b), IND(C(T2, a * 16, b * 16), C(OL, 2 * h0, 2 * h1)), C("QS", a, b), OP.add)
             tr(C("K2T", a, b), C("K2", a, b))
@@ -598,12 +599,12 @@ def replay(nodes, order, lat_x, lat_s, cost):
 
 def tuned(nodes):
     n = len(nodes)
-    c1 = [nd["cost"] for nd in nodes]
-    c2 = [nd["cost"] * (1.5 if nd["eng"] == "P" else 1) + (30 if nd["eng"] in "VA" else 0) for nd in nodes]
+    c1 = [nd["cost"] * 1.15 + 20 if nd["eng"] in "VAP" else nd["cost"] for nd in nodes]
+    c2 = [nd["cost"] * (1.3 if nd["eng"] in "VAP" else 1) for nd in nodes]
 
     def value(b):
-        o, e = schedule(nodes, b, 150, 100, c1)
-        return max(e) + replay(nodes, o, 250, 150, c2), o
+        o, e = schedule(nodes, b, 290, 240, c1)
+        return max(e) + replay(nodes, o, 170, 120, c2), o
     rng = np.random.default_rng(0)
     bias = np.zeros(n)
     best = value(bias)

import numpy as np
from concourse.bass import DstId, RemoteDMATransfer
from concourse.mybir import AluOpType as OP
from concourse.mybir import ActivationFunctionType as AF

V, G, W, NR = 2048, 256, 3840, 8
PL0, OWN, GH, GR, TB1, WEND = 1, 2064, 4112, 5904, 7952, 11792
F32, BF, F16, I32, U16 = "float32", "bfloat16", "float16", "int32", "uint16"
SMALL = {"MK": 16, "WF": 16, "W25": 16, "WI": 64, "KM": 16, "FM": 80, "THR": 16, "RE": 64, "LV": 80, "OV": 64, "E1": 64,
         "PLW": 64, "GD": 64, "AM": 48, "GO": 16, "VAL": 64, "FZ": 16, "OO": 64, "O2": 64, "RKC": 16, "PAY": 32, "O4": 48}
BUFS = {
    I32: {"NB": V, "PT": V, "REQ": 32, "TH": 4, "PB": 8, "RI": 64, "PX0": 256, "PX1": 256, "CST": 256, "MI": 16,
          "I2": 32, "BI": 16, "I3": 32, "E2": 64, "E3": 64, "DD": 32, "O3": 32},
    BF: {"WIN": WEND, "Y": V, "XT": W, "I1": 128, "IK": 128, "IH": 128, "SW": (4, 128), "I21": 128, "SELD": 64,
         "MKD": 16, "TRI": 128, "ONE": 128, "SELF": 16, "SELC": 8, "RMIN": 128, "EE": 32, "IA": 240, "P0": 4096, "P1": 4096,
         "T0": 4096, "T1": 4096, "SG": 256, "OH0": 256, "OH1": 256, "OB": 112, "X0": 256, "X1": 256, "ZW": 1024, "OA": 8192,
         "ZF": 256, "TS": 128, "TW": 240, "M01": 128, "PR": 256, "IND": 128, "LVB": 128, "INP": 128, "N01": 128,
         "ZO": (128, 16), "ZZ": 128, "PIB": 256},
    U16: {"LAND": 224, "MSG": 32, "L16": 64, "L8": 8, "LK": 4, "BL": 320, "QL": 160, "Q0": 256, "Q1": 256, "OL0": 32,
          "OL1": 32, "CL": 8, "IX": 128},
    F16: {"LOW": 128, "QF": 256, "ZV": 1024},
    F32: {"SF": sum(SMALL.values()), "PF": 8, "DM": 128, "JF": 256, "IF": 128, "SELP": 8, "RMAX": 128, "R8": 128, "DI": 128,
          "JI": 128, "KB": 128, "K0": 128, "K1": 128, "THC": 1, "QS": 256, "SU": 256, "KEY": (8, 2, 16), "KT": 256, "SC": 256,
          "K2": 256, "K2T": 256, "SC2": 256, "PS": 256, "FH": (5, 2, 2, 8), "PH": (4, 2, 2, 8), "CI": 128, "RK": 128,
          "PTS": 128, "X3": 128, "OS": (2, 4, 16)},
}
SCRATCH = {n: ("sbuf", [128] + (list(s) if isinstance(s, tuple) else [s]), d) for d, b in BUFS.items() for n, s in b.items()}
SCRATCH.update({n: ("psum", [128, 512], F32) for n in ("S0", "S1", "F1", "TT", "TM", "OC", "SM")})
SCRATCH["QQ"] = ("psum", [128, 16, 2, 16], F32)
SEMAPHORES = ["sv", "sa", "sp", "sg", "arr0", "arr1", "out0", "out1"] + ["d%d" % i for i in range(12)]
HUGE = 2.0 ** 58
BAN = 2.0 ** 24
PE_CYC, SLACK, TRIES = 0.5, 80, 1200
BLOCKS = (((0, 2), (2, 5)), ((0, 4), (4, 8)))
DVE_CHUNKS = {(0, 0): (1, 3), (1, 0): (1, 3)}
ORDER = {}


def build(g, T, rank, topo):
    nodes = []
    sgs = []
    hist = {}
    grids = {}
    place = {}
    for n_, w_ in SMALL.items():
        place[n_] = sum(SMALL[m_] for m_ in place)

    def A(name, *idx):
        if name in SMALL:
            a, b, st = (idx[0] if idx else slice(None)).indices(SMALL[name])
            name, idx = "SF", (slice(place[name] + a, place[name] + b, st if st > 1 else None),)
        where, shape, d = SCRATCH[name]
        if name not in grids:
            grids[name] = np.arange(int(np.prod(shape[1:]))).reshape(shape[1:])
        sel = grids[name][idx].ravel() if idx else grids[name].ravel()
        bits = np.zeros(grids[name].size, np.uint8)
        bits[sel] = 1
        m = int.from_bytes(np.packbits(bits).tobytes(), "big")
        ap = T[name][(slice(None),) + idx] if idx else T[name][:]
        return {"ap": ap, "acc": [(name, m)], "n": len(sel), "two": d in (BF, F16, U16), "ps": where == "psum", "ind": False}

    def C(name, a, b=None, st=None):
        return A(name, slice(a, a + 1 if b is None else b, st))

    def D(name, a, n):
        return C(name, a, a + n)

    ALL = slice(None)

    def IND(win, off):
        return {"ap": win["ap"].indirect(off["ap"]), "acc": win["acc"] + off["acc"], "n": off["n"] * 16,
                "two": False, "ps": False, "ind": True}

    def node(eng, cost, emit, rd, wr, sem=None, cnt=0, after=()):
        k = len(nodes)
        deps = {}
        acc = [(name, m, w) for ops, w in ((rd, False), (wr, True)) for o in ops if isinstance(o, dict) for name, m in o["acc"]]
        for name, m, w in acc:
            ps = SCRATCH[name][0] == "psum"
            for j, mj, wj in hist.get(name, ()):
                if ps and nodes[j]["eng"] != eng:
                    deps[j] = True
                elif (w or wj) and (m & mj):
                    deps[j] = deps.get(j, False) or not (ps and eng == "P")
        for j in after:
            deps.setdefault(j, False)
        lab = wr[0]["acc"][0][0] if wr and isinstance(wr[0], dict) else "-"
        nodes.append({"eng": eng, "cost": cost, "emit": emit, "deps": deps, "sem": sem, "cnt": cnt, "lab": lab})
        for name, m, w in acc:
            h = hist.setdefault(name, [])
            if w and SCRATCH[name][0] != "psum":
                h[:] = [e for e in h if e[1] & ~m]
            h.append((k, m, w))
        return k

    def ap(o):
        return o["ap"] if isinstance(o, dict) else o

    def vcost(out, a, both=False):
        if a["ind"]:
            return 60 + 1.5 * a["n"]
        return max(64, a["n"] * (2 if both else 0.5 if (out["two"] and a["two"]) else 1))

    def cp(out, a):
        return node("V", vcost(out, a), lambda: g.vector.tensor_copy(out["ap"], a["ap"]), [a], [out])

    def tt(out, a, b, op):
        c = vcost(out, a, True) if not (a["ps"] or b["ps"]) else max(64, a["n"])
        return node("V", c, lambda: g.vector.tensor_tensor(out["ap"], a["ap"], b["ap"], op), [a, b], [out])

    def ts(out, a, s1, op0, s2=None, op1=None):
        def emit():
            if op1 is None:
                return g.vector.tensor_scalar(out["ap"], a["ap"], ap(s1), None, op0)
            return g.vector.tensor_scalar(out["ap"], a["ap"], ap(s1), ap(s2), op0, op1)
        return node("V", vcost(out, a), emit, [a, s1, s2], [out])

    def ms(out, v):
        return node("V", vcost(out, out), lambda: g.vector.memset(out["ap"], v), [], [out])

    def scan(out, d0, d1, op0, op1):
        return node("V", vcost(out, d1), lambda: g.vector.tensor_tensor_scan(out["ap"], d0["ap"], d1["ap"], 0.0, op0, op1), [d0, d1], [out])

    def tr(out, a):
        return node("V", vcost(out, a), lambda: g.vector.transpose(out["ap"], a["ap"]), [a], [out])

    def rec(out, a):
        return node("V", 230 + 6 * a["n"], lambda: g.vector.reciprocal(out["ap"], a["ap"]), [a], [out])

    def act(out, a, func, bias=0.0, scale=1.0, extra=0, after=()):
        c = (80 + 1.5 * a["n"] if a["ind"] else max(64, a["n"]) + 20) + extra
        return node("A", c, lambda: g.scalar.activation(out["ap"], a["ap"], func, bias=ap(bias), scale=ap(scale)), [a, bias, scale], [out], after=after)

    def gather(eng, out, src, after=()):
        return cp(out, src) if eng == "V" else act(out, src, AF.Copy, after=after)

    def mm(lst, after=()):
        def emit():
            for o, l, r, st, sp in lst:
                ins = g.tensor.matmul(o["ap"], l["ap"], r["ap"], st, sp)
            return ins
        c = sum(max(min(64, l["n"]), r["n"]) * (1 if l["two"] else 4) for o, l, r, st, sp in lst) * PE_CYC + 40
        return node("P", c, emit, [e[1] for e in lst] + [e[2] for e in lst], [e[0] for e in lst], after=after)

    def grp(lst):
        return [(o, l, r, i == 0, i == len(lst) - 1) for i, (o, l, r) in enumerate(lst)]

    def iota(out, pat, base, cm=0):
        def emit():
            if SCRATCH[out["acc"][0][0]][2] == I32:
                return g.iota(out["ap"], pat, base, cm)
            return g.iota(out["ap"], pat, base, cm, allow_small_or_imprecise_dtypes=True)
        return node("G", 160 + 2 * out["n"], emit, [], [out])

    def fill(out, v):
        return iota(out, [[0, out["n"]]], v)

    def dma(out, a, sem, cost, cnt=16, behind=None):
        wr = [out] if isinstance(out, dict) else []
        return node("S", cost, lambda: g.sync.dma_start(ap(out), ap(a)).then_inc(T.sem[sem], 16), [a, behind], wr, sem=sem, cnt=cnt)

    def ways(src):
        used, res, load = 0, {}, None
        for m in sorted({topo.mask(src, c) for c in T.cores if c != src}, key=lambda x: bin(x).count("1")):
            to = [c for c in T.cores if c != src and topo.mask(src, c) == m]
            free = [e for e in topo.engines(src, to[0]) if not used >> e & 1]
            load = load or len(to) / len(free)
            while len(free) > 1 and 2 * len(to) / len(free) <= load:
                free = free[::2]
            for c in to:
                res[c] = sum(1 << e for e in free)
            used |= m
        return res

    def send(src, dst_of, arr, out, landing, cost):
        me = T.cores[rank]
        mine = ways(me)
        tf = []
        for mk in sorted(set(mine.values())):
            qs = [q for q in range(NR) if mine.get(T.cores[q]) == mk]
            tf.append(RemoteDMATransfer(dst_ids=[DstId(rid=topo.addr(T.cores[q])[0], pnc=topo.addr(T.cores[q])[1]) for q in qs],
                                        dma_engine_mask=mk, remote_sem=T.sem[arr], src=src["ap"], dsts=[dst_of(q) for q in qs]))
        sent = sum(bin(mk).count("1") for mk in set(mine.values()))
        k = node("G", 300, lambda: g.remote_dma_fused(tf, local_sem=T.sem[out]), [src], [], sem=out, cnt=sent)
        got = sum(bin(ways(c)[me]).count("1") for c in T.cores if c != me)
        node("X", cost, None, [], [landing], sem=arr, cnt=got, after=[k])

    dma(D("WIN", OWN, G), T.x[:, 0:G], "d0", 2200)
    dma(C("REQ", 0, 18), T.req[:], "d1", 2200)
    dma(A("NB"), T.nb[:], "d2", 6000)
    dma(C("WIN", OWN + G, OWN + V), T.x[:, G:V], "d3", 7000)
    dma(C("TH", 0, 1), T.th[:], "d4", 7000)
    dma(A("PT"), T.pt[:], "d5", 4500, behind=A("NB"))
    iota(C("PB", 4), [[0, 1]], 0, 1)
    iota(A("JF"), [[1, 256]], 0)
    iota(A("DM"), [[1, 128]], 0, -1)
    iota(A("THR"), [[128, 2], [0, 8]], -128, 1)
    send(D("WIN", OWN, G), lambda q: T.WIN[:, GH + ((q - rank) % NR - 1) * G:GH + ((q - rank) % NR) * G],
         "arr0", "out0", C("WIN", GH, GR), 6000)
    iota(C("KT", 0, 128), [[512, 4], [32, 16], [0, 2]], 0)
    fill(A("X0"), 0)
    iota(A("RMAX"), [[0, 8], [300, 16]], 0)
    for n_ in ("ZZ", "PR", "OH0", "PS", "X1", "OH1"):
        fill(A(n_), 0)
    iota(A("DI"), [[0, 16], [1, 8]], 8)
    iota(A("JI"), [[0, 8], [1, 16]], -16)
    iota(C("X3", 0, 64), [[16, 8], [1, 8]], 0, -1)
    iota(A("ZO"), [[0, 128], [0, 16]], 0)
    ms(C("WIN", 0, 16), 0.0)
    ms(C("WIN", 2048, OWN), 0.0)
    dma(D("WIN", PL0, V), T.plans[:], "d6", 3500, behind=A("PT"))
    for q in range(NR):
        d = (rank - q) % NR
        dma(D("WIN", GR + q * G, G), D("WIN", GH + (d - 1) * G if d else OWN, G), "d7", 2000, 16 * NR)

    pi = C("PB", 4)
    ts(C("PB", 0), pi, 15, OP.bitwise_and)
    ts(C("PB", 1), pi, 4, OP.logical_shift_right)
    ts(C("PB", 2), pi, 4, OP.logical_shift_right, 1, OP.bitwise_and)
    ts(C("PB", 3), pi, 3, OP.logical_shift_right, 1, OP.bitwise_and)
    cp(C("PF", 0, 4), C("PB", 0, 4))
    cF, gF, gbF, x3F, ngbF, qbF, lowF = (C("PF", i) for i in range(7))
    ts(ngbF, gbF, -1.0, OP.mult, 1.0, OP.add)
    ts(qbF, cF, -1.0 / 16, OP.mult, (15 * 4096 + 2048) / 65536, OP.add)
    ts(lowF, gbF, 16.0, OP.mult, cF, OP.add)
    ms(C("PF", 7), 0.25)
    ms(C("RI", 0, 32), V)
    cp(C("RI", 0, 5), C("REQ", 0, 5))
    cp(C("RI", 16, 20), C("REQ", 5, 9))
    ms(C("QL", 8, 16), 0)
    cp(C("QL", 0, 5), C("REQ", 0, 5))
    cp(C("QL", 8, 12), C("REQ", 5, 9))
    ts(C("RI", 8, 16), C("RI", 0, 8), 4, OP.logical_shift_right)
    ts(C("RI", 24, 32), C("RI", 16, 24), 4, OP.logical_shift_right)
    cp(C("BL", 0, 32), C("RI", 0, 32))
    cp(C("BL", 160, 168), C("REQ", 9, 17))
    ts(C("RI", 40, 48), C("REQ", 9, 17), 4, OP.logical_shift_right)
    cp(C("BL", 168, 176), C("RI", 40, 48))
    cp(C("RI", 48), C("REQ", 17))
    cp(C("QL", 80, 89), C("REQ", 9, 18))
    ts(A("I1"), A("DM"), 0.0, OP.is_equal)
    ts(A("IK"), A("I1"), 2048.0, OP.mult)
    ts(A("I21"), A("I1"), 2.0 ** 21, OP.mult)
    ts(A("IH"), A("I1"), HUGE, OP.mult, HUGE, OP.mult)
    ts(A("LOW"), C("KT", 0, 128), lowF, OP.add)
    for u in range(2):
        for w in range(2):
            ts(A("SW", 2 * u + w), A("DM"), 16.0 * (w - u), OP.is_equal, gbF if u else ngbF, OP.mult)
    ts(A("THC"), C("TH", 0), -2048.0, OP.mult, -2047.5, OP.add)
    ms(A("RMIN"), 0.0)
    ms(C("RMIN", 0, 128, 16), 2.0 ** 30)
    ms(A("MI"), 0)
    ms(A("I3"), 0)
    ts(A("MKD"), C("JF", 0, 16), -8.0, OP.add, cF, OP.is_equal)
    ts(A("SELD"), C("X3", 0, 64), 0.0, OP.is_equal)
    ts(A("IA"), C("JF", 0, 240), 1.0, OP.add)
    ts(A("MK"), C("JF", 0, 16), cF, OP.is_equal)
    act(C("TS", 0, 16), A("THR"), AF.Exp, scale=-0.875 * float(np.log(2.0)), extra=1600)
    for b in range(16):
        if b % 8 < 5:
            act(C("XT", b, W, 16), A("IA"), AF.Identity, scale=C("MK", b))
        else:
            ts(C("XT", b, W, 16), A("IA"), C("MK", b), OP.mult)
    ts(C("EE", 1, 32, 2), A("MK"), BAN, OP.mult)
    ts(C("EE", 0, 32, 2), A("MK"), 2 * BAN, OP.mult)
    ts(C("SELF", 0, 8), C("JF", 0, 8), gF, OP.is_equal)
    ts(C("SELF", 8, 16), C("SELF", 0, 8), cF, OP.mult)
    ts(A("SELP"), C("SELF", 0, 8), 1 / BAN, OP.mult)
    ts(A("SELC"), C("SELF", 8, 16), 1 / BAN, OP.mult)
    cp(A("WF"), C("TS", 0, 16))
    ts(A("W25"), A("WF"), 2.5, OP.mult)
    rec(C("WI", 0, 16), A("WF"))
    act(C("WI", 16, 32), C("WI", 0, 16), AF.Copy)
    act(C("WI", 32, 64), C("WI", 0, 32), AF.Copy)
    ms(A("ONE"), 1.0)
    ms(A("R8"), 1.0)
    ms(C("R8", 0, 128, 8), 0.0)
    ts(C("TW", 128, 240), C("ONE", 0, 112), HUGE, OP.mult, HUGE, OP.mult)
    ms(C("LV", 0, 16), 1.0)
    act(A("IF"), A("I1"), AF.Copy)
    ts(A("TRI"), A("DM"), 0.0, OP.is_gt)
    ts(A("N01"), A("I1"), -16.0, OP.mult)
    tt(A("TRI"), A("TRI"), A("N01"), OP.add)
    cp(A("L16"), C("JF", 0, 64))
    ts(A("L8"), C("JF", 0, 8), 2.0, OP.mult, x3F, OP.add)
    ts(A("LK"), C("JF", 0, 4), 0.0, OP.mult, cF, OP.add)
    act(A("KB"), C("JF", 0, 128), AF.Identity, bias=cF, scale=16.0)
    ts(A("KM"), C("KB", 0, 16), float(GR + rank * G), OP.add)
    ts(A("K0"), A("KB"), float(OWN), OP.add)
    ts(A("K1"), A("KB"), float(TB1), OP.add)

    def halves(H):
        return [(0, 16)] if H == 8 else [(0, H), (8, 8 + H)]

    def comers(r, k):
        H = 8 if r else 5
        s = (r * 5 + k) * 32
        X = "X%d" % (k % 2)
        for l in range(2):
            act(D(X, l * 128, 16 * H), IND(A("XT"), D("BL", s + 16 * l, H)), AF.Copy)
        lst = []
        for l in range(2):
            lst += grp([(D("F1", 256 + l * 16, 16), D(X, l * 128, 128), A("SELF"))])
            if k < 4:
                lst += grp([(D("F1", l * 128, 128), D(X, l * 128, 128), A("I1"))])
        mm(lst)
        act(A("FH", k), C("F1", 256, 288), AF.Copy)
        if k < 4:
            for l in range(2):
                ts(D("ZW", k * 256 + l * 128, 128), D("F1", l * 128, 128), 1.0, OP.min, C("WF", l * 8), OP.mult)

    def conflicts(r, k):
        H = 8 if r else 5
        s = (r * 5 + k) * 32
        X = "X%d" % (k % 2)
        fm = D("FM", k * 16, 16)
        tt(fm, A("FH", k, ALL, 0), D("LV", k * 16, 16), OP.mult)
        if k == 4:
            return
        tt(A("THR"), fm, A("W25"), OP.mult)
        for c in range(16):
            ts(D("OA", (k * 16 + c) * 128, 128), C("IA", 0, 128), C("FM", k * 16 + c), OP.is_equal)
        last = mm([(C("TT", 0, 128), A("IH"), A("M01" if r or k else "ZZ"), True, False)])
        for h in range(2):
            last = mm([(D("TT", gg * 16, 16), D("OA", (k * 16 + h * 8 + gg) * 128, 128), D("ZW", k * 256 + h * 128 + gg * 16, 16),
                        False, h == 1 and gg == 7) for gg in range(8)], after=[last])
        act(A("TS"), C("TT", 0, 128), AF.Copy)
        mm(grp([(C("TM", 0, 128), A("TS"), A("I1"))]))
        act(C("TW", 0, 128), C("TM", 0, 128), AF.Copy)
        if k < 3:
            act(A("M01"), A("TS"), AF.Sign)
        for l in range(2):
            tt(D("PR", l * 128, 16 * H), IND(A("TW"), D("BL", s + 16 * l + 8, H)), D(X, l * 128, 16 * H), OP.mult)
        mm(grp([(C("SM", 0, 8), C("PR", 0, 128), C("SELF", 0, 8))]) + grp([(C("SM", 8, 16), C("PR", 128, 256), C("SELF", 0, 8))]))
        tt(D("RE", k * 16, 16), C("SM", 0, 16), A("THR"), OP.is_lt)

    def step(r, k):
        H = 8 if r else 5
        n = 32 * H
        s = (r * 5 + k) * 32
        sq = (r * 5 + k) * 16
        e = str(k % 2)
        Q, PX, P, T2, OL, OH = "Q" + e, "PX" + e, "P" + e, "T" + e, "OL" + e, "OH" + e
        OHP = "OH%d" % ((k + 1) % 2)
        tab = D("WIN", TB1 if r else OWN, W)
        if r and not k:
            act(A("OB"), IND(A("EE"), C("CL", 0, 7)), AF.Copy)
        for bi, (h0, h1) in enumerate(BLOCKS[r]):
            S, m = "S%d" % bi, 32 * (h1 - h0)
            for l in range(2):
                cp(C(Q, h0 * 32 + l, h1 * 32, 2), IND(A("NB"), C("QL", sq + 8 * l + h0, sq + 8 * l + h1)))
            last = mm([(C(S, 0, m), A("I1"), C("LOW", 0, m), True, False)])
            for h in range(h0, h1):
                gather("V" if h in DVE_CHUNKS.get((r, k), ()) else "A", D(P, h * 512, 512), IND(tab, D(Q, h * 32, 32)),
                       after=sgs[-1:] if h == h0 + 1 else ())
                tr(D(T2, h * 512, 512), D(P, h * 512, 512))
                if h % 2 or h == h1 - 1:
                    u = h - h % 2
                    last = mm([(C(S, (u - h0) * 32, (h + 1 - h0) * 32), A("IK"), C(P, u * 512 + i, h * 512 + 512, 16), False,
                                not (r or k) and h == h1 - 1 and i == 15) for i in range(16)], after=[last])
            if k:
                mm([(C(S, l, m, 2), A("SW", 2 * l + gb), C(OHP, gb * 128 + h0 * 16, gb * 128 + h1 * 16), False, l + gb == 2)
                    for l in range(2) for gb in range(2)], after=[last])
            elif r:
                u = max(h0, 1)
                mm([(C(S, (u - h0) * 32 + 1, m, 2), A("I1"), C("OB", (u - 1) * 16, (h1 - 1) * 16), False, True)], after=[last])
            sg = C("SG", h0 * 32, h1 * 32)
            act(sg, C(S, 0, m), AF.Sign, bias=A("THC"))
            sgs.append(act(C("SU", h0 * 32, h1 * 32), sg, AF.Identity, bias=C("PF", 7), scale=2.0 ** 22 - 0.25))
        ts(C("QF", 0, n), C(Q, 0, n), -2048.0, OP.add)
        lst = []
        for gb in range(2):
            lst += grp([(A("QQ", slice(0, H), gb), A("SW", 2 * gb + l), C("QF", l, n, 2)) for l in range(2)])
        mm(lst)
        act(C("QS", 0, n), A("QQ", slice(0, H)), AF.Identity, bias=qbF, scale=1 / 65536)
        for a, b in halves(H):
            ts(C(PX, a * 16, b * 16), IND(A("PT"), C("QL", sq + a, sq + b)), 4194304.0, OP.add)
        for l in range(2):
            ts(C("CST", l, n, 2), D(PX, l * 128, 16 * H), 1023 << 11, OP.bitwise_and)
        for bi, (h0, h1) in enumerate(BLOCKS[r]):
            S, m, a, b = "S%d" % bi, 32 * (h1 - h0), 32 * h0, 32 * h1
            tt(D(S, 256, m), C(S, 0, m), C("CST", a, b), OP.add)
            for l in range(2):
                tt(A("KEY", slice(h0, h1), l), C(S, 256 + l, 256 + m, 2), C("SU", a + l, b, 2), OP.add)
            tr(C("KT", a, b), A("KEY", slice(h0, h1)))
            scan(C("SC", a, b), C("RMIN", 0, m), C("KT", a, b), OP.add, OP.min)
            mi, i2 = C("MI", 2 * h0, 2 * h1), C("I2", 2 * h0, 2 * h1)
            ts(mi, C("SC", a + 15, b, 16), 2.0, OP.mult)
            ts(i2, mi, 1, OP.logical_shift_right, 2047, OP.bitwise_and)
            cp(C(OL, 2 * h0, 2 * h1), i2)
            tt(C("K2", a, b), IND(C(T2, a * 16, b * 16), C(OL, 2 * h0, 2 * h1)), C("QS", a, b), OP.add)
            tr(C("K2T", a, b), C("K2", a, b))
            scan(C("SC2", a, b), C("RMAX", 0, m), C("K2T", a, b), OP.min, OP.max)
            ts(C("BI", 2 * h0, 2 * h1), C("SC2", a + 15, b, 16), 65536.0, OP.mult)
            if (r, k) != (1, 3):
                ts(C("I3", 2 * h0, 2 * h1), C("BI", 2 * h0, 2 * h1), 4095, OP.bitwise_and)
            if k < 3:
                for l in range(2):
                    ts(C("QL", sq + 16 + 8 * l + h0, sq + 16 + 8 * l + h1), C("I3", 2 * h0 + l, 2 * h1, 2), V - 1.0, OP.min)
        ts(D("I3", 16, 2 * H), C("BI", 0, 2 * H), 4 if k < 3 else 8, OP.logical_shift_right, 255 if k < 3 else 15, OP.bitwise_and)
        for l in range(2):
            cp(D("BL", s + 32 + 16 * l, 16), C("I3", l, 32, 2))
        ts(C("I2", 16, 32), A("MI"), 31, OP.bitwise_and)
        for gb in range(2):
            cp(D(OL, 16 + 8 * gb, 8), C("I2", 16 + gb, 32, 2))
        for a, b in halves(H):
            act(C(OH, a * 16, b * 16), IND(A("EE"), C(OL, 16 + a, 16 + b)), AF.Copy)
        lst = []
        for l in range(2):
            lst += grp([(D("OC", l * 128, 16 * H), A("SW", 2 * l + gb), D(OH, gb * 128, 16 * H)) for gb in range(2)])
        mm(lst)
        for a, b in halves(H):
            tt(C("PS", a * 16, b * 16), C("OC", a * 16, b * 16), C(PX, a * 16, b * 16), OP.mult)
        lst = []
        for l in range(2):
            lst += grp([(D("OC", 256 + l * 16, 8), D("PS", l * 128, 128), A("SELP"))])
            for gb in range(2):
                lst += grp([(C("OC", 264 + l * 16 + gb, 272 + l * 16, 2), D(OH, gb * 128, 128), C("SELC", l, 8, 2))])
        mm(lst)
        act(A("PH", k), C("OC", 256, 288), AF.Copy)
        ts(D("OV", k * 16, 16), A("PH", k, ALL, 0), 8388608.0, OP.is_ge)

    def table():
        tt(A("VAL"), IND(A("GO"), A("LK")), A("PLW"), OP.mult)
        for k in range(4):
            tt(D("ZV", k * 256, 256), IND(A("VAL"), D("L16", k * 16, 16)), D("ZW", k * 256, 256), OP.mult)
        last = mm([(C("TT", 0, 128), A("I1"), A("ZZ"), True, False)])
        for k in range(4):
            last = mm([(D("TT", gg * 16, 16), D("OA", (k * 16 + l * 8 + gg) * 128, 128), D("ZV", k * 256 + l * 128 + gg * 16, 16),
                        False, k == 3 and l == 1 and gg == 7) for gg in range(8) for l in range(2)], after=[last])
        act(A("PTS"), C("TT", 0, 128), AF.Copy)
        act(A("N01"), C("TT", 0, 128), AF.Relu, bias=C("LV", 0), scale=-1.0)
        mm(grp([(C("TM", 0, 128), A("PTS"), A("IF")), (C("TM", 0, 128), A("N01"), A("I21"))]))

    def index(out, a, b, keep):
        tt(C("X3", a, b), C("TM", a, b), keep, OP.min)
        cp(out, C("X3", a, b))

    def finish(r):
        H = 8 if r else 5
        s = (r * 5 + 4) * 32 + 8
        act(A("E1"), A("OV"), AF.Identity, bias=C("LV", 0), scale=-0.5)
        tt(A("E2"), A("PH", ALL, ALL, 0), A("E1"), OP.mult)
        ts(A("E3"), A("E2"), 2047, OP.bitwise_and)
        ts(A("E1"), A("E3"), 1.0, OP.add)
        tt(A("PLW"), A("E1"), A("RE"), OP.mult)
        tt(A("PLW"), A("PLW"), A("WI"), OP.mult)
        tt(A("GD"), A("RE"), C("LV", 16, 80), OP.subtract)
        tt(C("GD", 0, 32), C("GD", 0, 32), C("GD", 32, 64), OP.add)
        tt(C("GD", 0, 16), C("GD", 0, 16), C("GD", 16, 32), OP.add)
        tt(C("AM", 16, 32), C("FM", 16, 32), C("FM", 32, 48), OP.max)
        tt(C("AM", 32, 48), C("AM", 16, 32), C("FM", 48, 64), OP.max)
        ts(C("DD", 16, 32), C("AM", 32, 48), -1.0, OP.add)
        ts(C("DD", 0, 16), C("DD", 16, 32), 4, OP.arith_shift_right)
        tt(A("INP"), IND(C("DD", 0, 16), A("L8")), A("DI"), OP.is_equal)
        act(A("LVB"), IND(C("LV", 64, 80), A("L8")), AF.Copy)
        for l in range(2):
            gather("AV"[l], D("PR", l * 128, 16 * H), IND(A("MKD"), D("BL", s + 16 * l, H)))
        last = mm([(C("S1", 0, 128), A("I1"), A(n_), i == 0, False) for i, n_ in enumerate(("INP", "INP", "LVB"))])
        mm([(D("S1", 64 * l, 64), D("PR", l * 128, 128), A("SELD"), False, l == 1) for l in range(2)], after=[last])
        ts(A("IND"), C("S1", 0, 128), 2.0, OP.is_ge)
        mm(grp([(C("S0", 0, 64), A("TRI"), C("IND", 0, 64))]) +
           grp([(C("S0", 64, 128), A("ONE"), C("IND", 0, 64)), (C("S0", 64, 128), A("TRI"), C("IND", 64, 128))]))
        tt(A("CI"), C("S0", 0, 128), A("IND"), OP.mult)
        scan(A("RK"), A("R8"), A("CI"), OP.mult, OP.add)
        tt(A("GO"), C("RK", 7, 128, 8), C("GD", 0, 16), OP.is_lt)
        table()
        if r:
            for h in range(2):
                index(D("IX", h * 64, 64), h * 64, h * 64 + 64, D("K1", h * 64, 64))
            for c in range(8):
                gather("AVAVAVAV"[c], D("Y", c * G, G), IND(C("WIN", 0, TB1 + V), D("IX", c * 16, 16)))
            for c in range(4):
                dma(T.y[:, c * 512:c * 512 + 512], D("Y", c * 512, 512), "d%d" % (8 + c), 2000)
            return
        am = C("AM", 0, 16)
        tt(am, C("AM", 32, 48), C("FM", 64, 80), OP.max)
        ts(C("DD", 16, 32), am, -1.0, OP.add)
        ts(A("OO"), C("FM", 16, 80), 128.0, OP.is_gt)
        tt(A("OS", 0), A("OO"), A("FH", slice(1, 5), ALL, 1), OP.mult)
        tt(A("OS", 1), A("OO"), A("PH", ALL, ALL, 1), OP.mult)
        tt(A("O2"), A("OS", ALL, slice(0, 2)), A("OS", ALL, slice(2, 4)), OP.add)
        tt(C("O4", 0, 16), C("O2", 0, 16), C("O2", 16, 32), OP.add)
        tt(C("PAY", 16, 32), C("O2", 32, 48), C("O2", 48, 64), OP.add)
        ts(C("O4", 16, 32), am, 1.0, OP.max)
        rec(C("OO", 0, 16), C("O4", 16, 32))
        tt(C("O4", 16, 32), C("O4", 0, 16), C("OO", 0, 16), OP.mult)
        cp(C("O3", 0, 16), C("O4", 16, 32))
        ts(C("O3", 16, 32), C("DD", 16, 32), 15, OP.bitwise_and)
        ts(C("O4", 32, 48), C("O3", 16, 32), 16.0, OP.mult, 1.0, OP.add)
        tt(C("PAY", 0, 16), C("O4", 32, 48), C("O3", 0, 16), OP.add)
        for f in range(2):
            tt(C("PIB", f, 256, 2), IND(D("PAY", f * 16, 16), A("L8")), A("IND"), OP.mult)
        act(A("RKC"), C("RK", 7, 128, 8), AF.Copy)
        for l in range(2):
            tt(D("SG", 128 * l, 128), IND(A("RKC"), D("L16", 8 * l, 8)), A("JI"), OP.is_equal)
            act(A("ZO", slice(64 * l, 64 * l + 64, 9)), D("SG", 128 * l, 128), AF.Copy)
        mm(grp([(C("SM", 32, 48), A("ZO", slice(c * 8, c * 8 + 8)), D("PIB", c * 16, 16)) for c in range(16)]))
        ts(C("O4", 0, 8), C("SM", 32, 48, 2), 0.0, OP.is_equal, 2049.0, OP.mult)
        tt(C("O4", 8, 16), C("SM", 32, 48, 2), C("O4", 0, 8), OP.add)
        ts(C("MSG", 16, 24), C("O4", 8, 16), -1.0, OP.add)
        cp(C("MSG", 24, 32), C("SM", 33, 48, 2))
        index(C("MSG", 0, 16), 0, 16, A("KM"))
        send(A("MSG"), lambda q: T.LAND[:, ((rank - q) % NR - 1) * 32:((rank - q) % NR) * 32], "arr1", "out1", A("LAND"), 5000)
        index(A("IX"), 0, 128, A("K0"))
        for c in range(8):
            gather("AVAVAAVA"[c], D("WIN", TB1 + c * G, G), IND(C("WIN", 0, TB1), D("IX", c * 16, 16)))
        tt(A("FZ"), C("RE", 0, 16), A("GO"), OP.is_gt)
        tt(A("ZF"), IND(A("FZ"), C("L16", 0, 16)), C("ZW", 0, 256), OP.mult)
        lst = []
        for gg in range(8):
            lst += grp([(D("TT", gg * 16, 16), D("OA", (l * 8 + gg) * 128, 128), D("ZF", l * 128 + gg * 16, 16)) for l in range(2)])
        mm(lst)
        act(A("M01"), C("TT", 0, 128), AF.Sign)
        ts(C("QL", 89, 96), C("LAND", 16, 224, 33), V - 1.0, OP.min)
        cp(C("CL", 0, 7), C("LAND", 24, 224, 33))
        cp(C("RI", 49, 56), C("LAND", 16, 224, 33))
        ts(C("RI", 56, 64), C("RI", 48, 56), 4, OP.logical_shift_right)
        cp(C("BL", 176, 192), C("RI", 48, 64))
        for d in range(1, NR):
            gather("VA"[d % 2], D("WIN", TB1 + V + (NR - d - 1) * G, G), IND(C("WIN", 0, TB1), D("LAND", (d - 1) * 32, 16)))

    for r in range(2):
        for k in range(4):
            comers(r, k)
            conflicts(r, k)
            step(r, k)
            tt(D("LV", k * 16 + 16, 16), D("RE", k * 16, 16), D("OV", k * 16, 16), OP.mult)
        if not r:
            comers(r, 4)
            conflicts(r, 4)
        finish(r)
    return nodes


def schedule(nodes, bias, lat_x, lat_s, cost):
    n = len(nodes)
    eng = [nd["eng"] for nd in nodes]
    succ = [[] for _ in range(n)]
    for k, nd in enumerate(nodes):
        for j, hard in nd["deps"].items():
            succ[j].append((k, (lat_s if eng[j] == eng[k] else lat_x) if hard else 0))
    pr = [0.0] * n
    for k in range(n - 1, -1, -1):
        pr[k] = cost[k] + max([pr[s] + la for s, la in succ[k]], default=0)
    pr = [pr[k] + bias[k] for k in range(n)]
    left = [len(nd["deps"]) for nd in nodes]
    ready_at = [0.0] * n
    end = [0.0] * n
    free = {e: 0.0 for e in "VAPGSX"}
    pool = {e: [k for k in range(n) if eng[k] == e and not left[k]] for e in "VAPGSX"}
    order = {e: [] for e in "VAPGSX"}
    queued = {e: [k for k in range(n) if eng[k] == e] for e in "GSX"}
    for _ in range(n):
        best = None
        for e in "VAPGSX":
            if pool[e]:
                if e in "GSX":
                    k = queued[e][len(order[e])]
                    if k not in pool[e]:
                        continue
                    t = max(free[e], ready_at[k])
                else:
                    t = max(free[e], min(ready_at[k] for k in pool[e]))
                    k = max((k for k in pool[e] if ready_at[k] <= t + SLACK), key=lambda k: pr[k])
                    t = max(t, ready_at[k])
                if best is None or t < best[0]:
                    best = (t, e, k)
        t, e, k = best
        pool[e].remove(k)
        order[e].append(k)
        end[k] = t + cost[k]
        free[e] = t + (60 if e in "SX" else cost[k])
        for s, la in succ[k]:
            ready_at[s] = max(ready_at[s], end[k] + la)
            left[s] -= 1
            if not left[s]:
                pool[eng[s]].append(s)
    return order, end


def replay(nodes, order, lat_x, lat_s, cost):
    end = {}
    pos = {e: 0 for e in order}
    free = {e: 0.0 for e in order}
    while len(end) < len(nodes):
        for e in order:
            while pos[e] < len(order[e]):
                k = order[e][pos[e]]
                deps = nodes[k]["deps"]
                if any(j not in end for j in deps):
                    break
                t = max([free[e]] + [end[j] + ((lat_s if nodes[j]["eng"] == e else lat_x) if h else 0) for j, h in deps.items()])
                end[k] = t + cost[k]
                free[e] = t + (60 if e in "SX" else cost[k])
                pos[e] += 1
    return max(end.values())


def tuned(nodes):
    n = len(nodes)
    c1 = [nd["cost"] * 1.15 + 20 if nd["eng"] in "VAP" else nd["cost"] for nd in nodes]
    c2 = [nd["cost"] * (1.3 if nd["eng"] in "VAP" else 1) for nd in nodes]

    def value(b):
        o, e = schedule(nodes, b, 290, 240, c1)
        return max(e) + replay(nodes, o, 170, 120, c2), o
    rng = np.random.default_rng(0)
    bias = np.zeros(n)
    best = value(bias)
    for _ in range(TRIES):
        c = bias.copy()
        i = int(rng.integers(n))
        d = rng.normal() * 1500
        if rng.integers(2):
            c[i:i + int(rng.integers(1, 40))] += d
        else:
            for k in range(max(0, i - 60), min(n, i + 60)):
                if nodes[k]["lab"] == nodes[i]["lab"]:
                    c[k] += d
        v = value(c)
        if v[0] <= best[0]:
            best, bias = v, c
    return best[1]


def rank_program(g, core, T, topo):
    rank = T.rank_of(core)
    if rank is None:
        return
    nodes = build(g, T, rank, topo)
    if "o" not in ORDER:
        ORDER["o"] = tuned(nodes)
    order = ORDER["o"]
    queue = {"V": g.vector, "A": g.scalar, "P": g.tensor, "G": g, "S": g.sync}
    own = {"V": "sv", "A": "sa", "P": "sp", "G": "sg"}
    needed = set()
    for nd in nodes:
        if nd["eng"] != "X":
            needed.update(j for j, hard in nd["deps"].items() if hard)
    mark = {}
    total = {}
    for e in "VAPG":
        for k in order[e]:
            if nodes[k]["sem"] is None and k in needed:
                total[own[e]] = total.get(own[e], 0) + 1
                mark[k] = (own[e], total[own[e]])
    for k, nd in enumerate(nodes):
        if nd["sem"] is not None:
            mark[k] = (nd["sem"], nd["cnt"])
            total[nd["sem"]] = nd["cnt"]
    for e in "SGVAP":
        seen = {}
        for k in order[e]:
            want = {}
            for j, hard in nodes[k]["deps"].items():
                if hard:
                    want[mark[j][0]] = max(want.get(mark[j][0], 0), mark[j][1])
            for s, c in want.items():
                if seen.get(s, 0) < c:
                    queue[e].wait_ge(T.sem[s], c)
                    seen[s] = c
            ins = nodes[k]["emit"]()
            if nodes[k]["sem"] is None and k in mark:
                ins.then_inc(T.sem[mark[k][0]], 1)
        if e == "S":
            for s, c in total.items():
                if seen.get(s, 0) < c:
                    g.sync.wait_ge(T.sem[s], c)
